import numpy as np
import ml_dtypes


def mxq(x, axis, fmt="e4m3"):
    dtype, down = {"e4m3": (ml_dtypes.float8_e4m3fn, 7), "e5m2": (ml_dtypes.float8_e5m2, 14)}[fmt]
    v = np.moveaxis(np.asarray(x, np.float32).astype(ml_dtypes.bfloat16).astype(np.float64), axis, -1)
    blocks = v.reshape(v.shape[:-1] + (-1, 32))
    amax = np.abs(blocks).max(-1, keepdims=True)
    byte = np.maximum(np.where(amax > 0, np.frexp(amax)[1] - 1 + 127, 0) - down, 1)
    scale = np.exp2(byte - 127.0)
    codes = (blocks / scale).astype(np.float32).astype(dtype).astype(np.float64)
    return np.moveaxis((codes * scale).reshape(v.shape), -1, axis)


WIDE = False


def mx_kscale(k):
    if not WIDE:
        return np.ones(k)
    levels = np.array([10, -10, 5, -5, 0])
    if k % 512:
        return np.exp2(np.random.permutation(np.resize(levels, k // 32))).repeat(32)
    a = np.empty((k // 512, 16))
    for p in range(k // 512):
        a[p, :8] = np.random.permutation(np.resize(levels, 8))
        for g in range(8):
            far = levels[np.abs(levels - a[p, g]) >= 10]
            a[p, g + 8] = far[np.random.randint(len(far))]
    return np.exp2(a.ravel()).repeat(32)


def f64(x):
    return np.asarray(x).astype(np.float64)


def striped(idx):
    return np.tile(np.asarray(idx).reshape(-1, 16).T, (8, 1)).astype(np.uint16)


def unstriped(offs):
    return offs[:16].T.reshape(-1).astype(np.int64)


B, N, T, D, NQ = 1, 512, 2048, 512, 256


def setup_inputs():
    n = np.random.standard_normal
    idx = np.random.permutation(T)[:B * N]
    idx2 = np.random.permutation(1024)[:B * N]
    s = mx_kscale(D)[:, None]
    return {
        "qT": (n((B, D, NQ)) * s * (1.00 / np.sqrt(D))).astype(np.float32),
        "kT": (np.clip(np.round(n((D, T)) * 16), -64, 64) / 16 / s).astype(np.float32),
        "rT": (np.clip(np.round(n((D, 1024)) * 16), -64, 64) / 16 / s).astype(np.float32),
        "ob": (0.5 * n((B, NQ, 1))).astype(np.float32),
        "offs": striped(idx),
        "offs2": striped(idx2),
    }


def reference(qT, kT, rT, ob, offs, offs2):
    idx = unstriped(offs)
    idx2 = unstriped(offs2)
    pick = lambda x, which: x[:, which].reshape(x.shape[0], B, -1).transpose(1, 0, 2)
    kg = pick(f64(kT), idx)
    rg = pick(f64(rT), idx2)
    ug = mxq(kg - rg, 1, "e4m3")
    qq = mxq(f64(qT), 1, "e4m3")
    a = qq.transpose(0, 2, 1) @ ug
    y = np.maximum(a + f64(ob), 0.0)
    return y

@@ -1,0 +1,131 @@
+from contextlib import ExitStack
+
+import concourse.mybir as mybir
+
+D, T, S, N, NQ = 512, 2048, 1024, 512, 256
+FLOPS = 2 * D * N * NQ
+
+F32 = mybir.dt.float32
+BF16 = mybir.dt.bfloat16
+U32 = mybir.dt.uint32
+U16 = mybir.dt.uint16
+U8 = mybir.dt.uint8
+FP8X4 = mybir.dt.float8_e4m3fn_x4
+ALU = mybir.AluOpType
+ACT = mybir.ActivationFunctionType
+
+P = 128
+PACK = 4
+HALF = N // 2
+CW = 128
+NCH = N // CW
+
+
+def tile_attend_pre_edge_f_topk_kernel(tc, qT, kT, rT, ob, offs, offs2, out):
+    nc = tc.nc
+    with ExitStack() as ctx:
+        lists = ctx.enter_context(tc.tile_pool(name="lists", bufs=1))
+        keep = ctx.enter_context(tc.tile_pool(name="keep", bufs=1))
+        psum = ctx.enter_context(tc.psum_pool(name="psum", bufs=1))
+
+        k_list = lists.tile([P, N // 16], U16, name="k_list")
+        r_list = lists.tile([P, N // 16], U16, name="r_list")
+        r_rows = rT.rearrange("(p t) s -> p t s", t=PACK)
+        k_rows = kT.rearrange("(p t) s -> p t s", t=PACK)
+        r_tab = [keep.tile([P, 2, S], F32, name=f"r_tab{j}") for j in range(2)]
+        k_tab = [keep.tile([P, T], F32, name=f"k_tab{t}") for t in range(PACK)]
+        q_raw = keep.tile([P, PACK, NQ], F32, name="q_raw")
+        bias = [keep.tile([P, 1], F32, name=f"bias{h}") for h in range(2)]
+
+        nc.sync.dma_start(r_tab[0][:], r_rows[:, 0:2, :])
+        nc.sync.dma_start(r_list[:], offs2)
+        nc.sync.dma_start(r_tab[1][:], r_rows[:, 2:4, :])
+        nc.sync.dma_start(k_list[:], offs)
+        for t in range(PACK):
+            nc.sync.dma_start(k_tab[t][:], k_rows[:, t, :])
+        nc.sync.dma_start(q_raw[:], qT[0].rearrange("(p t) q -> p t q", t=PACK))
+        for h in range(2):
+            nc.sync.dma_start(bias[h][:], ob[0, h * P:(h + 1) * P, :])
+
+        r_g = [keep.tile([P, N], F32, name=f"r_g{t}") for t in range(PACK)]
+        k_g = [keep.tile([P, N], F32, name=f"k_g{t}") for t in range(PACK - 1)]
+        k_last = [keep.tile([P, HALF], F32, name=f"k_last{j}") for j in range(2)]
+        diff_lo = keep.tile([P, 2, N], BF16, name="diff_lo")
+        diff_hi = [keep.tile([P, 2, HALF], BF16, name=f"diff_hi{j}") for j in range(2)]
+        u = [keep.tile([P, CW, PACK], BF16, name=f"u{c}", align_bytes=64) for c in range(NCH)]
+        u_codes = [keep.tile([P, CW], U32, name=f"u_codes{c}", align_bytes=64) for c in range(NCH)]
+        u_scales = [keep.tile([P, CW], U8, name=f"u_scales{c}", align_bytes=64) for c in range(NCH)]
+        q_bf = [keep.tile([P, P, PACK], BF16, name=f"q_bf{h}", align_bytes=64) for h in range(2)]
+        q_codes = [keep.tile([P, P], U32, name=f"q_codes{h}", align_bytes=64) for h in range(2)]
+        q_scales = [keep.tile([P, P], U8, name=f"q_scales{h}", align_bytes=64) for h in range(2)]
+        res = [keep.tile([P, 2, CW], F32, name=f"res{c}") for c in range(NCH)]
+        out_v = out[0].rearrange("(h p) n -> p h n", p=P)
+
+        for t in range(PACK):
+            nc.vector.tensor_copy(r_g[t][:], r_tab[t // 2][:, t % 2, :].indirect(r_list[:]))
+        for t in range(2):
+            nc.vector.tensor_copy(k_g[t][:], k_tab[t][:].indirect(k_list[:]))
+            nc.vector.tensor_tensor(diff_lo[:, t, :], k_g[t][:], r_g[t][:], ALU.subtract)
+        for c in range(NCH):
+            nc.scalar.copy(u[c][:, :, 0:2], diff_lo[:, :, c * CW:(c + 1) * CW].rearrange("p t n -> p n t"))
+        nc.vector.tensor_copy(k_g[2][:], k_tab[2][:].indirect(k_list[:]))
+        for j in range(2):
+            cols = slice(j * HALF, (j + 1) * HALF)
+            nc.vector.tensor_tensor(diff_hi[j][:, 0, :], k_g[2][:, cols], r_g[2][:, cols], ALU.subtract)
+
+        for j in range(2):
+            nc.vector.tensor_copy(k_last[j][:], k_tab[3][:].indirect(k_list[:, j * (HALF // 16):(j + 1) * (HALF // 16)]))
+        for j in range(2):
+            cols = slice(j * HALF, (j + 1) * HALF)
+            nc.vector.tensor_tensor(diff_hi[j][:, 1, :], k_last[j][:], r_g[3][:, cols], ALU.subtract)
+
+        for h in range(2):
+            nc.scalar.copy(
+                q_bf[h][:].rearrange("p (c i) t -> p c t i", i=4),
+                q_raw[:, :, h * P:(h + 1) * P].rearrange("p t (c i) -> p c t i", i=4),
+            )
+
+        def place(c):
+            j, o = divmod(c * CW, HALF)
+            nc.vector.tensor_copy(u[c][:, :, 2:4], diff_hi[j][:, :, o:o + CW].rearrange("p t n -> p n t"))
+
+        def quant_u(c):
+            nc.vector.quantize_mx(out=u_codes[c][:].bitcast(FP8X4), scales=u_scales[c][:], in_=u[c][:].rearrange("p n t -> p (n t)"))
+
+        def quant_q(h):
+            nc.vector.quantize_mx(out=q_codes[h][:].bitcast(FP8X4), scales=q_scales[h][:], in_=q_bf[h][:].rearrange("p n t -> p (n t)"))
+
+        def project(c, h):
+            acc = psum.tile([P, CW], F32, name=f"acc{c}_{h}")
+            nc.tensor.matmul_mx(out=acc[:], lhsT=q_codes[h][:].bitcast(FP8X4), lhsT_scale=q_scales[h][:],
+                                rhs=u_codes[c][:].bitcast(FP8X4), rhs_scale=u_scales[c][:], start=True, stop=True)
+            if c == NCH - 1 and h == 1:
+                nc.vector.tensor_scalar(res[c][:, h, :], acc[:], bias[h][:], 0.0, ALU.add, ALU.max)
+            else:
+                nc.scalar.activation(res[c][:, h, :], acc[:], ACT.Relu, bias=bias[h][:])
+
+        def store(c):
+            nc.sync.dma_start(out_v[:, :, c * CW:(c + 1) * CW], res[c][:])
+
+        place(0)
+        place(1)
+        quant_q(0)
+        quant_u(0)
+        project(0, 0)
+        place(2)
+        quant_q(1)
+        project(0, 1)
+        store(0)
+        quant_u(1)
+        project(1, 0)
+        project(1, 1)
+        store(1)
+        place(3)
+        quant_u(2)
+        project(2, 0)
+        project(2, 1)
+        store(2)
+        quant_u(3)
+        project(3, 0)
+        project(3, 1)
+        store(3)

@@ -34,7 +34,8 @@ def tile_attend_pre_edge_f_topk_kernel(tc, qT, kT, rT, ob, offs, offs2, out):
         k_rows = kT.rearrange("(p t) s -> p t s", t=PACK)
         r_tab = [keep.tile([P, 2, S], F32, name=f"r_tab{j}") for j in range(2)]
         k_tab = [keep.tile([P, T], F32, name=f"k_tab{t}") for t in range(PACK)]
-        q_raw = keep.tile([P, PACK, NQ], F32, name="q_raw")
+        stage = keep.tile([P, HALF // 2 + PACK * NQ], F32, name="stage")
+        q_raw = stage[:, HALF // 2:].rearrange("p (t q) -> p t q", t=PACK)
         bias = [keep.tile([P, 1], F32, name=f"bias{h}") for h in range(2)]
 
         nc.sync.dma_start(r_tab[0][:], r_rows[:, 0:2, :])
@@ -43,7 +44,7 @@ def tile_attend_pre_edge_f_topk_kernel(tc, qT, kT, rT, ob, offs, offs2, out):
         nc.sync.dma_start(k_list[:], offs)
         for t in range(PACK):
             nc.sync.dma_start(k_tab[t][:], k_rows[:, t, :])
-        nc.sync.dma_start(q_raw[:], qT[0].rearrange("(p t) q -> p t q", t=PACK))
+        nc.sync.dma_start(q_raw, qT[0].rearrange("(p t) q -> p t q", t=PACK))
         for h in range(2):
             nc.sync.dma_start(bias[h][:], ob[0, h * P:(h + 1) * P, :])
 
@@ -51,13 +52,12 @@ def tile_attend_pre_edge_f_topk_kernel(tc, qT, kT, rT, ob, offs, offs2, out):
         k_g = [keep.tile([P, N], F32, name=f"k_g{t}") for t in range(PACK - 1)]
         k_last = [keep.tile([P, HALF], F32, name=f"k_last{j}") for j in range(2)]
         diff_lo = keep.tile([P, 2, N], BF16, name="diff_lo")
-        diff_hi = [keep.tile([P, 2, HALF], BF16, name=f"diff_hi{j}") for j in range(2)]
-        u = [keep.tile([P, CW, PACK], BF16, name=f"u{c}", align_bytes=64) for c in range(NCH)]
-        u_codes = [keep.tile([P, CW], U32, name=f"u_codes{c}", align_bytes=64) for c in range(NCH)]
-        u_scales = [keep.tile([P, CW], U8, name=f"u_scales{c}", align_bytes=64) for c in range(NCH)]
-        q_bf = [keep.tile([P, P, PACK], BF16, name=f"q_bf{h}", align_bytes=64) for h in range(2)]
-        q_codes = [keep.tile([P, P], U32, name=f"q_codes{h}", align_bytes=64) for h in range(2)]
-        q_scales = [keep.tile([P, P], U8, name=f"q_scales{h}", align_bytes=64) for h in range(2)]
+        diff_hi0 = keep.tile([P, 2, HALF], BF16, name="diff_hi0")
+        diff_hi = [diff_hi0[:], stage[:, 0:HALF].bitcast(BF16).rearrange("p (t n) -> p t n", t=2)]
+        widths = [CW + P if c < 2 else CW for c in range(NCH)]
+        grouped = [keep.tile([P, w, PACK], BF16, name=f"grouped{c}", align_bytes=64) for c, w in enumerate(widths)]
+        codes = [keep.tile([P, w], U32, name=f"codes{c}", align_bytes=64) for c, w in enumerate(widths)]
+        scales = [keep.tile([P, w], U8, name=f"scales{c}", align_bytes=64) for c, w in enumerate(widths)]
         res = [keep.tile([P, 2, CW], F32, name=f"res{c}") for c in range(NCH)]
         out_v = out[0].rearrange("(h p) n -> p h n", p=P)
 
@@ -67,7 +67,7 @@ def tile_attend_pre_edge_f_topk_kernel(tc, qT, kT, rT, ob, offs, offs2, out):
             nc.vector.tensor_copy(k_g[t][:], k_tab[t][:].indirect(k_list[:]))
             nc.vector.tensor_tensor(diff_lo[:, t, :], k_g[t][:], r_g[t][:], ALU.subtract)
         for c in range(NCH):
-            nc.scalar.copy(u[c][:, :, 0:2], diff_lo[:, :, c * CW:(c + 1) * CW].rearrange("p t n -> p n t"))
+            nc.scalar.copy(grouped[c][:, 0:CW, 0:2], diff_lo[:, :, c * CW:(c + 1) * CW].rearrange("p t n -> p n t"))
         nc.vector.tensor_copy(k_g[2][:], k_tab[2][:].indirect(k_list[:]))
         for j in range(2):
             cols = slice(j * HALF, (j + 1) * HALF)
@@ -75,31 +75,29 @@ def tile_attend_pre_edge_f_topk_kernel(tc, qT, kT, rT, ob, offs, offs2, out):
 
         for j in range(2):
             nc.vector.tensor_copy(k_last[j][:], k_tab[3][:].indirect(k_list[:, j * (HALF // 16):(j + 1) * (HALF // 16)]))
-        for j in range(2):
+
+        def last_diff(j):
             cols = slice(j * HALF, (j + 1) * HALF)
             nc.vector.tensor_tensor(diff_hi[j][:, 1, :], k_last[j][:], r_g[3][:, cols], ALU.subtract)
 
         for h in range(2):
             nc.scalar.copy(
-                q_bf[h][:].rearrange("p (c i) t -> p c t i", i=4),
+                grouped[h][:, CW:, :].rearrange("p (c i) t -> p c t i", i=4),
                 q_raw[:, :, h * P:(h + 1) * P].rearrange("p t (c i) -> p c t i", i=4),
             )
 
         def place(c):
             j, o = divmod(c * CW, HALF)
-            nc.vector.tensor_copy(u[c][:, :, 2:4], diff_hi[j][:, :, o:o + CW].rearrange("p t n -> p n t"))
+            nc.vector.tensor_copy(grouped[c][:, 0:CW, 2:4], diff_hi[j][:, :, o:o + CW].rearrange("p t n -> p n t"))
 
-        def quant_u(c):
-            nc.vector.quantize_mx(out=u_codes[c][:].bitcast(FP8X4), scales=u_scales[c][:], in_=u[c][:].rearrange("p n t -> p (n t)"))
-
-        def quant_q(h):
-            nc.vector.quantize_mx(out=q_codes[h][:].bitcast(FP8X4), scales=q_scales[h][:], in_=q_bf[h][:].rearrange("p n t -> p (n t)"))
+        def quant(c):
+            nc.vector.quantize_mx(out=codes[c][:].bitcast(FP8X4), scales=scales[c][:], in_=grouped[c][:].rearrange("p n t -> p (n t)"))
 
         def project(c, h):
             acc = psum.tile([P, CW], F32, name=f"acc{c}_{h}")
-            nc.tensor.matmul_mx(out=acc[:], lhsT=q_codes[h][:].bitcast(FP8X4), lhsT_scale=q_scales[h][:],
-                                rhs=u_codes[c][:].bitcast(FP8X4), rhs_scale=u_scales[c][:], start=True, stop=True)
-            if c == NCH - 1 and h == 1:
+            nc.tensor.matmul_mx(out=acc[:], lhsT=codes[h][:, CW:].bitcast(FP8X4), lhsT_scale=scales[h][:, CW:],
+                                rhs=codes[c][:, 0:CW].bitcast(FP8X4), rhs_scale=scales[c][:, 0:CW], start=True, stop=True)
+            if c >= 2 and h == 1:
                 nc.vector.tensor_scalar(res[c][:, h, :], acc[:], bias[h][:], 0.0, ALU.add, ALU.max)
             else:
                 nc.scalar.activation(res[c][:, h, :], acc[:], ACT.Relu, bias=bias[h][:])
@@ -107,25 +105,25 @@ def tile_attend_pre_edge_f_topk_kernel(tc, qT, kT, rT, ob, offs, offs2, out):
         def store(c):
             nc.sync.dma_start(out_v[:, :, c * CW:(c + 1) * CW], res[c][:])
 
+        last_diff(0)
         place(0)
         place(1)
-        quant_q(0)
-        quant_u(0)
+        quant(0)
         project(0, 0)
-        place(2)
-        quant_q(1)
+        last_diff(1)
+        quant(1)
         project(0, 1)
         store(0)
-        quant_u(1)
         project(1, 0)
         project(1, 1)
         store(1)
+        place(2)
         place(3)
-        quant_u(2)
+        quant(2)
+        quant(3)
         project(2, 0)
         project(2, 1)
         store(2)
-        quant_u(3)
         project(3, 0)
         project(3, 1)
         store(3)

@@ -1,6 +1,7 @@
 from contextlib import ExitStack
 
 import concourse.mybir as mybir
+from concourse.masks import make_identity
 
 D, T, S, N, NQ = 512, 2048, 1024, 512, 256
 FLOPS = 2 * D * N * NQ
@@ -61,6 +62,15 @@ def tile_attend_pre_edge_f_topk_kernel(tc, qT, kT, rT, ob, offs, offs2, out):
         res = [keep.tile([P, 2, CW], F32, name=f"res{c}") for c in range(NCH)]
         out_v = out[0].rearrange("(h p) n -> p h n", p=P)
 
+        ident = keep.tile([P, P], F32, name="ident")
+        make_identity(nc, ident[:])
+        warm = psum.tile([P, 4, P], F32, name="warm", tag="last_bank")
+
+        def warm_up(src, count):
+            blocks = src.shape[1] // P
+            for i in range(count):
+                nc.tensor.transpose(warm[:, i % 4, :], src[:, (i % blocks) * P:(i % blocks + 1) * P], ident[:])
+
         for t in range(PACK):
             nc.vector.tensor_copy(r_g[t][:], r_tab[t // 2][:, t % 2, :].indirect(r_list[:]))
         for t in range(2):
@@ -68,6 +78,7 @@ def tile_attend_pre_edge_f_topk_kernel(tc, qT, kT, rT, ob, offs, offs2, out):
             nc.vector.tensor_tensor(diff_lo[:, t, :], k_g[t][:], r_g[t][:], ALU.subtract)
         for c in range(NCH):
             nc.scalar.copy(grouped[c][:, 0:CW, 0:2], diff_lo[:, :, c * CW:(c + 1) * CW].rearrange("p t n -> p n t"))
+        warm_up(k_tab[2][:], 18)
         nc.vector.tensor_copy(k_g[2][:], k_tab[2][:].indirect(k_list[:]))
         for j in range(2):
             cols = slice(j * HALF, (j + 1) * HALF)
@@ -75,8 +86,14 @@ def tile_attend_pre_edge_f_topk_kernel(tc, qT, kT, rT, ob, offs, offs2, out):
 
         for j in range(2):
             nc.vector.tensor_copy(k_last[j][:], k_tab[3][:].indirect(k_list[:, j * (HALF // 16):(j + 1) * (HALF // 16)]))
+        warm_up(k_last[0][:], 4)
+        warm_up(k_last[1][:], 8)
 
-        def last_diff(j):
+        def last_diff(c):
+            j, o = divmod(c * CW, HALF)
+            nc.vector.tensor_tensor(diff_hi[j][:, 1, o:o + CW], k_last[j][:, o:o + CW], r_g[3][:, c * CW:(c + 1) * CW], ALU.subtract)
+
+        def last_diff_half(j):
             cols = slice(j * HALF, (j + 1) * HALF)
             nc.vector.tensor_tensor(diff_hi[j][:, 1, :], k_last[j][:], r_g[3][:, cols], ALU.subtract)
 
@@ -94,7 +111,7 @@ def tile_attend_pre_edge_f_topk_kernel(tc, qT, kT, rT, ob, offs, offs2, out):
             nc.vector.quantize_mx(out=codes[c][:].bitcast(FP8X4), scales=scales[c][:], in_=grouped[c][:].rearrange("p n t -> p (n t)"))
 
         def project(c, h):
-            acc = psum.tile([P, CW], F32, name=f"acc{c}_{h}")
+            acc = psum.tile([P, CW], F32, name=f"acc{c}_{h}", tag="last_bank" if (c, h) == (NCH - 1, 1) else f"bank{c}_{h}")
             nc.tensor.matmul_mx(out=acc[:], lhsT=codes[h][:, CW:].bitcast(FP8X4), lhsT_scale=scales[h][:, CW:],
                                 rhs=codes[c][:, 0:CW].bitcast(FP8X4), rhs_scale=scales[c][:, 0:CW], start=True, stop=True)
             if c >= 2 and h == 1:
@@ -106,11 +123,12 @@ def tile_attend_pre_edge_f_topk_kernel(tc, qT, kT, rT, ob, offs, offs2, out):
             nc.sync.dma_start(out_v[:, :, c * CW:(c + 1) * CW], res[c][:])
 
         last_diff(0)
+        last_diff(1)
         place(0)
         place(1)
         quant(0)
         project(0, 0)
-        last_diff(1)
+        last_diff_half(1)
         quant(1)
         project(0, 1)
         store(0)

@@ -1,7 +1,6 @@
 from contextlib import ExitStack
 
 import concourse.mybir as mybir
-from concourse.masks import make_identity
 
 D, T, S, N, NQ = 512, 2048, 1024, 512, 256
 FLOPS = 2 * D * N * NQ
@@ -9,6 +8,7 @@ FLOPS = 2 * D * N * NQ
 F32 = mybir.dt.float32
 BF16 = mybir.dt.bfloat16
 U32 = mybir.dt.uint32
+I32 = mybir.dt.int32
 U16 = mybir.dt.uint16
 U8 = mybir.dt.uint8
 FP8X4 = mybir.dt.float8_e4m3fn_x4
@@ -35,8 +35,8 @@ def tile_attend_pre_edge_f_topk_kernel(tc, qT, kT, rT, ob, offs, offs2, out):
         k_rows = kT.rearrange("(p t) s -> p t s", t=PACK)
         r_tab = [keep.tile([P, 2, S], F32, name=f"r_tab{j}") for j in range(2)]
         k_tab = [keep.tile([P, T], F32, name=f"k_tab{t}") for t in range(PACK)]
-        stage = keep.tile([P, HALF // 2 + PACK * NQ], F32, name="stage")
-        q_raw = stage[:, HALF // 2:].rearrange("p (t q) -> p t q", t=PACK)
+        stage = keep.tile([P, P + PACK * NQ], F32, name="stage", align_bytes=64)
+        q_raw = stage[:, P:].rearrange("p (t q) -> p t q", t=PACK)
         bias = [keep.tile([P, 1], F32, name=f"bias{h}") for h in range(2)]
 
         nc.sync.dma_start(r_tab[0][:], r_rows[:, 0:2, :])
@@ -49,99 +49,87 @@ def tile_attend_pre_edge_f_topk_kernel(tc, qT, kT, rT, ob, offs, offs2, out):
         for h in range(2):
             nc.sync.dma_start(bias[h][:], ob[0, h * P:(h + 1) * P, :])
 
-        r_g = [keep.tile([P, N], F32, name=f"r_g{t}") for t in range(PACK)]
-        k_g = [keep.tile([P, N], F32, name=f"k_g{t}") for t in range(PACK - 1)]
-        k_last = [keep.tile([P, HALF], F32, name=f"k_last{j}") for j in range(2)]
+        r_g = keep.tile([P, PACK, N], F32, name="r_g")
+        k_g = keep.tile([P, PACK, N], F32, name="k_g")
         diff_lo = keep.tile([P, 2, N], BF16, name="diff_lo")
-        diff_hi0 = keep.tile([P, 2, HALF], BF16, name="diff_hi0")
-        diff_hi = [diff_hi0[:], stage[:, 0:HALF].bitcast(BF16).rearrange("p (t n) -> p t n", t=2)]
-        widths = [CW + P if c < 2 else CW for c in range(NCH)]
-        grouped = [keep.tile([P, w, PACK], BF16, name=f"grouped{c}", align_bytes=64) for c, w in enumerate(widths)]
+        pairs = keep.tile([P, 2 * N * 2], BF16, name="pairs")
+        first = keep.tile([P, (CW + P) * PACK], BF16, name="first", align_bytes=64)
+        q_hi = keep.tile([P, P * PACK], BF16, name="q_hi", align_bytes=64)
+        words = CW * PACK // 2
+        grouped = [first[:]] + [stage[:, j * words:(j + 1) * words].bitcast(BF16) for j in range(NCH - 1)] + [q_hi[:]]
+        widths = [CW + P] + [CW] * NCH
         codes = [keep.tile([P, w], U32, name=f"codes{c}", align_bytes=64) for c, w in enumerate(widths)]
         scales = [keep.tile([P, w], U8, name=f"scales{c}", align_bytes=64) for c, w in enumerate(widths)]
+        q_codes = [codes[0][:, CW:], codes[NCH][:]]
+        q_scales = [scales[0][:, CW:], scales[NCH][:]]
+        pair_lo = pairs[:, 0:2 * N]
+        pair_hi = pairs[:, 2 * N:].rearrange("p (n e) -> p n e", e=2)
+        pair_words = pairs[:].bitcast(U32).rearrange("p (u n) -> p u n", u=2)
         res = [keep.tile([P, 2, CW], F32, name=f"res{c}") for c in range(NCH)]
         out_v = out[0].rearrange("(h p) n -> p h n", p=P)
 
-        ident = keep.tile([P, P], F32, name="ident")
-        make_identity(nc, ident[:])
-        warm = psum.tile([P, 4, P], F32, name="warm", tag="last_bank")
+        def cols(c):
+            return slice(c * CW, (c + 1) * CW)
 
-        def warm_up(src, count):
-            blocks = src.shape[1] // P
-            for i in range(count):
-                nc.tensor.transpose(warm[:, i % 4, :], src[:, (i % blocks) * P:(i % blocks + 1) * P], ident[:])
+        def woven(c, first, run):
+            return grouped[c][:, first * PACK:(first + CW) * PACK].rearrange("p (c i t) -> p c t i", i=run, t=PACK)
+
+        def runs(planes, run):
+            return planes.rearrange("p t (c i) -> p c t i", i=run)
 
         for t in range(PACK):
-            nc.vector.tensor_copy(r_g[t][:], r_tab[t // 2][:, t % 2, :].indirect(r_list[:]))
-        for t in range(2):
-            nc.vector.tensor_copy(k_g[t][:], k_tab[t][:].indirect(k_list[:]))
-            nc.vector.tensor_tensor(diff_lo[:, t, :], k_g[t][:], r_g[t][:], ALU.subtract)
-        for c in range(NCH):
-            nc.scalar.copy(grouped[c][:, 0:CW, 0:2], diff_lo[:, :, c * CW:(c + 1) * CW].rearrange("p t n -> p n t"))
-        warm_up(k_tab[2][:], 18)
-        nc.vector.tensor_copy(k_g[2][:], k_tab[2][:].indirect(k_list[:]))
-        for j in range(2):
-            cols = slice(j * HALF, (j + 1) * HALF)
-            nc.vector.tensor_tensor(diff_hi[j][:, 0, :], k_g[2][:, cols], r_g[2][:, cols], ALU.subtract)
+            nc.vector.tensor_copy(r_g[:, t, :], r_tab[t // 2][:, t % 2, :].indirect(r_list[:]))
+        for t in range(PACK - 1):
+            nc.vector.tensor_copy(k_g[:, t, :], k_tab[t][:].indirect(k_list[:]))
+            if t < 2:
+                nc.vector.tensor_tensor(diff_lo[:, t, :], k_g[:, t, :], r_g[:, t, :], ALU.subtract)
+        nc.scalar.copy(pair_lo[:, 2 * CW:].rearrange("p (c i t) -> p c t i", i=4, t=2), runs(diff_lo[:, :, CW:], 4))
+        nc.vector.tensor_tensor(pair_hi[:, CW:, 0], k_g[:, 2, CW:], r_g[:, 2, CW:], ALU.subtract)
+        nc.scalar.copy(woven(0, 0, 4)[:, :, 0:2, :], runs(diff_lo[:, :, cols(0)], 4))
 
         for j in range(2):
-            nc.vector.tensor_copy(k_last[j][:], k_tab[3][:].indirect(k_list[:, j * (HALF // 16):(j + 1) * (HALF // 16)]))
-        warm_up(k_last[0][:], 4)
-        warm_up(k_last[1][:], 8)
+            nc.vector.tensor_copy(k_g[:, 3, j * HALF:(j + 1) * HALF],
+                                  k_tab[3][:].indirect(k_list[:, j * (HALF // 16):(j + 1) * (HALF // 16)]))
 
-        def last_diff(c):
-            j, o = divmod(c * CW, HALF)
-            nc.vector.tensor_tensor(diff_hi[j][:, 1, o:o + CW], k_last[j][:, o:o + CW], r_g[3][:, c * CW:(c + 1) * CW], ALU.subtract)
-
-        def last_diff_half(j):
-            cols = slice(j * HALF, (j + 1) * HALF)
-            nc.vector.tensor_tensor(diff_hi[j][:, 1, :], k_last[j][:], r_g[3][:, cols], ALU.subtract)
-
-        for h in range(2):
-            nc.scalar.copy(
-                grouped[h][:, CW:, :].rearrange("p (c i) t -> p c t i", i=4),
-                q_raw[:, :, h * P:(h + 1) * P].rearrange("p t (c i) -> p c t i", i=4),
-            )
-
-        def place(c):
-            j, o = divmod(c * CW, HALF)
-            nc.vector.tensor_copy(grouped[c][:, 0:CW, 2:4], diff_hi[j][:, :, o:o + CW].rearrange("p t n -> p n t"))
+        def weave_diff(c, t0):
+            nc.vector.tensor_tensor(woven(c, 0, 2)[:, :, t0:, :], runs(k_g[:, t0:, cols(c)], 2), runs(r_g[:, t0:, cols(c)], 2), ALU.subtract)
 
         def quant(c):
-            nc.vector.quantize_mx(out=codes[c][:].bitcast(FP8X4), scales=scales[c][:], in_=grouped[c][:].rearrange("p n t -> p (n t)"))
+            nc.vector.quantize_mx(out=codes[c][:].bitcast(FP8X4), scales=scales[c][:], in_=grouped[c])
 
         def project(c, h):
-            acc = psum.tile([P, CW], F32, name=f"acc{c}_{h}", tag="last_bank" if (c, h) == (NCH - 1, 1) else f"bank{c}_{h}")
-            nc.tensor.matmul_mx(out=acc[:], lhsT=codes[h][:, CW:].bitcast(FP8X4), lhsT_scale=scales[h][:, CW:],
+            acc = psum.tile([P, CW], F32, name=f"acc{c}_{h}", tag=f"bank{c}_{h}")
+            nc.tensor.matmul_mx(out=acc[:], lhsT=q_codes[h].bitcast(FP8X4), lhsT_scale=q_scales[h],
                                 rhs=codes[c][:, 0:CW].bitcast(FP8X4), rhs_scale=scales[c][:, 0:CW], start=True, stop=True)
-            if c >= 2 and h == 1:
+            if c >= 1 and h == 1:
                 nc.vector.tensor_scalar(res[c][:, h, :], acc[:], bias[h][:], 0.0, ALU.add, ALU.max)
             else:
                 nc.scalar.activation(res[c][:, h, :], acc[:], ACT.Relu, bias=bias[h][:])
 
         def store(c):
-            nc.sync.dma_start(out_v[:, :, c * CW:(c + 1) * CW], res[c][:])
+            nc.sync.dma_start(out_v[:, :, cols(c)], res[c][:])
 
-        last_diff(0)
-        last_diff(1)
-        place(0)
-        place(1)
+        def store_half(c, h):
+            nc.sync.dma_start(out_v[:, h, cols(c)], res[c][:, h, :])
+
+        nc.vector.tensor_tensor(pair_hi[:, cols(1), 1], k_g[:, 3, cols(1)], r_g[:, 3, cols(1)], ALU.subtract)
+        weave_diff(0, 2)
+        nc.vector.tensor_tensor(pair_hi[:, HALF:, 1], k_g[:, 3, HALF:], r_g[:, 3, HALF:], ALU.subtract)
+        nc.scalar.copy(woven(0, CW, 4), runs(q_raw[:, :, 0:P], 4))
+        nc.scalar.copy(woven(NCH, 0, 4), runs(q_raw[:, :, P:], 4))
+        for c in range(1, NCH - 1):
+            nc.scalar.copy(grouped[c].bitcast(U32).rearrange("p (c i u) -> p c u i", i=2, u=2), runs(pair_words[:, :, cols(c)], 2))
         quant(0)
+        quant(NCH)
+        nc.vector.tensor_copy(grouped[3].bitcast(I32).rearrange("p (c i u) -> p c u i", i=2, u=2),
+                              runs(pairs[:].bitcast(I32).rearrange("p (u n) -> p u n", u=2)[:, :, cols(3)], 2))
+        for c in range(1, NCH):
+            quant(c)
         project(0, 0)
-        last_diff_half(1)
-        quant(1)
+        store_half(0, 0)
         project(0, 1)
-        store(0)
-        project(1, 0)
-        project(1, 1)
-        store(1)
-        place(2)
-        place(3)
-        quant(2)
-        quant(3)
-        project(2, 0)
-        project(2, 1)
-        store(2)
-        project(3, 0)
-        project(3, 1)
-        store(3)
+        store_half(0, 1)
+        for c in range(1, NCH):
+            project(c, 0)
+            project(c, 1)
+            store(c)

@@ -64,7 +64,6 @@ def tile_attend_pre_edge_f_topk_kernel(tc, qT, kT, rT, ob, offs, offs2, out):
         q_scales = [scales[0][:, CW:], scales[NCH][:]]
         pair_lo = pairs[:, 0:2 * N]
         pair_hi = pairs[:, 2 * N:].rearrange("p (n e) -> p n e", e=2)
-        pair_words = pairs[:].bitcast(U32).rearrange("p (u n) -> p u n", u=2)
         res = [keep.tile([P, 2, CW], F32, name=f"res{c}") for c in range(NCH)]
         out_v = out[0].rearrange("(h p) n -> p h n", p=P)
 
@@ -117,12 +116,19 @@ def tile_attend_pre_edge_f_topk_kernel(tc, qT, kT, rT, ob, offs, offs2, out):
         nc.vector.tensor_tensor(pair_hi[:, HALF:, 1], k_g[:, 3, HALF:], r_g[:, 3, HALF:], ALU.subtract)
         nc.scalar.copy(woven(0, CW, 4), runs(q_raw[:, :, 0:P], 4))
         nc.scalar.copy(woven(NCH, 0, 4), runs(q_raw[:, :, P:], 4))
-        for c in range(1, NCH - 1):
-            nc.scalar.copy(grouped[c].bitcast(U32).rearrange("p (c i u) -> p c u i", i=2, u=2), runs(pair_words[:, :, cols(c)], 2))
+        late = stage[:, 0:(NCH - 1) * words]
+
+        def weave_words(copy, dtype, s0, s1):
+            copy(late[:, 2 * (s0 - CW):2 * (s1 - CW)].bitcast(dtype).rearrange("p (c i u) -> p c u i", i=4, u=2),
+                 runs(pairs[:].bitcast(dtype).rearrange("p (u n) -> p u n", u=2)[:, :, s0:s1], 4))
+
+        split = 2 * CW + CW // 2
+        weave_words(nc.scalar.copy, U32, CW, 2 * CW)
+        weave_words(nc.scalar.copy, U32, split, 3 * CW)
+        weave_words(nc.scalar.copy, U32, 3 * CW, N)
         quant(0)
         quant(NCH)
-        nc.vector.tensor_copy(grouped[3].bitcast(I32).rearrange("p (c i u) -> p c u i", i=2, u=2),
-                              runs(pairs[:].bitcast(I32).rearrange("p (u n) -> p u n", u=2)[:, :, cols(3)], 2))
+        weave_words(nc.vector.tensor_copy, I32, 2 * CW, split)
         for c in range(1, NCH):
             quant(c)
         project(0, 0)

@@ -33,37 +33,42 @@ def tile_attend_pre_edge_f_topk_kernel(tc, qT, kT, rT, ob, offs, offs2, out):
         r_list = lists.tile([P, N // 16], U16, name="r_list")
         r_rows = rT.rearrange("(p t) s -> p t s", t=PACK)
         k_rows = kT.rearrange("(p t) s -> p t s", t=PACK)
-        r_tab = [keep.tile([P, 2, S], F32, name=f"r_tab{j}") for j in range(2)]
+        q_rows = qT[0].rearrange("(p t) q -> p t q", t=PACK)
+        r_early = keep.tile([P, PACK - 1, S], F32, name="r_early")
+        r_last = keep.tile([P, S], F32, name="r_last")
         k_tab = [keep.tile([P, T], F32, name=f"k_tab{t}") for t in range(PACK)]
-        stage = keep.tile([P, P + PACK * NQ], F32, name="stage", align_bytes=64)
-        q_raw = stage[:, P:].rearrange("p (t q) -> p t q", t=PACK)
+        stage = [keep.tile([P, PACK * P], F32, name=f"stage{h}", align_bytes=64) for h in range(2)]
+        q_raw = [stage[h][:].rearrange("p (t q) -> p t q", t=PACK) for h in range(2)]
         bias = [keep.tile([P, 1], F32, name=f"bias{h}") for h in range(2)]
 
-        nc.sync.dma_start(r_tab[0][:], r_rows[:, 0:2, :])
+        nc.sync.dma_start(r_early[:], r_rows[:, 0:PACK - 1, :])
         nc.sync.dma_start(r_list[:], offs2)
-        nc.sync.dma_start(r_tab[1][:], r_rows[:, 2:4, :])
+        nc.sync.dma_start(k_tab[0][:], k_rows[:, 0, :])
         nc.sync.dma_start(k_list[:], offs)
-        for t in range(PACK):
+        for t in range(1, PACK):
             nc.sync.dma_start(k_tab[t][:], k_rows[:, t, :])
-        nc.sync.dma_start(q_raw, qT[0].rearrange("(p t) q -> p t q", t=PACK))
+        nc.sync.dma_start(r_last[:], r_rows[:, PACK - 1, :])
+        for h in range(2):
+            nc.sync.dma_start(q_raw[h], q_rows[:, :, h * P:(h + 1) * P])
         for h in range(2):
             nc.sync.dma_start(bias[h][:], ob[0, h * P:(h + 1) * P, :])
 
-        r_g = keep.tile([P, PACK, N], F32, name="r_g")
+        r_g = keep.tile([P, PACK - 1, N], F32, name="r_g")
         k_g = keep.tile([P, PACK, N], F32, name="k_g")
-        diff_lo = keep.tile([P, 2, N], BF16, name="diff_lo")
-        pairs = keep.tile([P, 2 * N * 2], BF16, name="pairs")
+        r3_g = r_g[:, 2, :]
+        pair_all = keep.tile([P, 2 * N * 2], BF16, name="pair_all")
         first = keep.tile([P, (CW + P) * PACK], BF16, name="first", align_bytes=64)
         q_hi = keep.tile([P, P * PACK], BF16, name="q_hi", align_bytes=64)
         words = CW * PACK // 2
-        grouped = [first[:]] + [stage[:, j * words:(j + 1) * words].bitcast(BF16) for j in range(NCH - 1)] + [q_hi[:]]
+        late = [stage[0][:, 0:words], stage[0][:, words:], stage[1][:, 0:words]]
+        grouped = [first[:]] + [w.bitcast(BF16) for w in late] + [q_hi[:]]
         widths = [CW + P] + [CW] * NCH
         codes = [keep.tile([P, w], U32, name=f"codes{c}", align_bytes=64) for c, w in enumerate(widths)]
         scales = [keep.tile([P, w], U8, name=f"scales{c}", align_bytes=64) for c, w in enumerate(widths)]
         q_codes = [codes[0][:, CW:], codes[NCH][:]]
         q_scales = [scales[0][:, CW:], scales[NCH][:]]
-        pair_lo = pairs[:, 0:2 * N]
-        pair_hi = pairs[:, 2 * N:].rearrange("p (n e) -> p n e", e=2)
+        pair_lo = pair_all[:, 0:2 * N].rearrange("p (n e) -> p n e", e=2)
+        pair_hi = pair_all[:, 2 * N:].rearrange("p (n e) -> p n e", e=2)
         res = [keep.tile([P, 2, CW], F32, name=f"res{c}") for c in range(NCH)]
         out_v = out[0].rearrange("(h p) n -> p h n", p=P)
 
@@ -76,22 +81,18 @@ def tile_attend_pre_edge_f_topk_kernel(tc, qT, kT, rT, ob, offs, offs2, out):
         def runs(planes, run):
             return planes.rearrange("p t (c i) -> p c t i", i=run)
 
-        for t in range(PACK):
-            nc.vector.tensor_copy(r_g[:, t, :], r_tab[t // 2][:, t % 2, :].indirect(r_list[:]))
         for t in range(PACK - 1):
+            nc.vector.tensor_copy(r_g[:, t, :], r_early[:, t, :].indirect(r_list[:]))
+        for t in range(PACK):
             nc.vector.tensor_copy(k_g[:, t, :], k_tab[t][:].indirect(k_list[:]))
-            if t < 2:
-                nc.vector.tensor_tensor(diff_lo[:, t, :], k_g[:, t, :], r_g[:, t, :], ALU.subtract)
-        nc.scalar.copy(pair_lo[:, 2 * CW:].rearrange("p (c i t) -> p c t i", i=4, t=2), runs(diff_lo[:, :, CW:], 4))
-        nc.vector.tensor_tensor(pair_hi[:, CW:, 0], k_g[:, 2, CW:], r_g[:, 2, CW:], ALU.subtract)
-        nc.scalar.copy(woven(0, 0, 4)[:, :, 0:2, :], runs(diff_lo[:, :, cols(0)], 4))
+        for t in range(2):
+            nc.gpsimd.tensor_tensor(pair_lo[:, CW:, t], k_g[:, t, CW:], r_g[:, t, CW:], ALU.subtract)
+        nc.gpsimd.tensor_tensor(woven(0, 0, 2)[:, :, 0:3, :], runs(k_g[:, 0:3, cols(0)], 2), runs(r_g[:, :, cols(0)], 2), ALU.subtract)
+        nc.gpsimd.tensor_tensor(pair_hi[:, CW:, 0], k_g[:, 2, CW:], r_g[:, 2, CW:], ALU.subtract)
 
-        for j in range(2):
-            nc.vector.tensor_copy(k_g[:, 3, j * HALF:(j + 1) * HALF],
-                                  k_tab[3][:].indirect(k_list[:, j * (HALF // 16):(j + 1) * (HALF // 16)]))
-
-        def weave_diff(c, t0):
-            nc.vector.tensor_tensor(woven(c, 0, 2)[:, :, t0:, :], runs(k_g[:, t0:, cols(c)], 2), runs(r_g[:, t0:, cols(c)], 2), ALU.subtract)
+        for c in range(NCH):
+            nc.vector.tensor_copy(r3_g[:, cols(c)], r_last[:].indirect(r_list[:, c * (CW // 16):(c + 1) * (CW // 16)]))
+        nc.gpsimd.tensor_tensor(first[:, 0:CW * PACK].rearrange("p (n t) -> p n t", t=PACK)[:, :, 3], k_g[:, 3, cols(0)], r3_g[:, cols(0)], ALU.subtract)
 
         def quant(c):
             nc.vector.quantize_mx(out=codes[c][:].bitcast(FP8X4), scales=scales[c][:], in_=grouped[c])
@@ -108,34 +109,21 @@ def tile_attend_pre_edge_f_topk_kernel(tc, qT, kT, rT, ob, offs, offs2, out):
         def store(c):
             nc.sync.dma_start(out_v[:, :, cols(c)], res[c][:])
 
-        def store_half(c, h):
-            nc.sync.dma_start(out_v[:, h, cols(c)], res[c][:, h, :])
+        def weave_words(copy, dtype, c):
+            copy(late[c - 1].bitcast(dtype).rearrange("p (c i u) -> p c u i", i=4, u=2),
+                 runs(pair_all[:].bitcast(dtype).rearrange("p (u n) -> p u n", u=2)[:, :, cols(c)], 4))
 
-        nc.vector.tensor_tensor(pair_hi[:, cols(1), 1], k_g[:, 3, cols(1)], r_g[:, 3, cols(1)], ALU.subtract)
-        weave_diff(0, 2)
-        nc.vector.tensor_tensor(pair_hi[:, HALF:, 1], k_g[:, 3, HALF:], r_g[:, 3, HALF:], ALU.subtract)
-        nc.scalar.copy(woven(0, CW, 4), runs(q_raw[:, :, 0:P], 4))
-        nc.scalar.copy(woven(NCH, 0, 4), runs(q_raw[:, :, P:], 4))
-        late = stage[:, 0:(NCH - 1) * words]
-
-        def weave_words(copy, dtype, s0, s1):
-            copy(late[:, 2 * (s0 - CW):2 * (s1 - CW)].bitcast(dtype).rearrange("p (c i u) -> p c u i", i=4, u=2),
-                 runs(pairs[:].bitcast(dtype).rearrange("p (u n) -> p u n", u=2)[:, :, s0:s1], 4))
-
-        split = 2 * CW + CW // 2
-        weave_words(nc.scalar.copy, U32, CW, 2 * CW)
-        weave_words(nc.scalar.copy, U32, split, 3 * CW)
-        weave_words(nc.scalar.copy, U32, 3 * CW, N)
+        for c in range(1, NCH):
+            nc.vector.tensor_tensor(pair_hi[:, cols(c), 1], k_g[:, 3, cols(c)], r3_g[:, cols(c)], ALU.subtract)
+        nc.scalar.copy(woven(0, CW, 4), runs(q_raw[0], 4))
+        nc.scalar.copy(woven(NCH, 0, 4), runs(q_raw[1], 4))
+        for c in range(1, NCH):
+            weave_words(nc.scalar.copy, U32, c)
         quant(0)
         quant(NCH)
-        weave_words(nc.vector.tensor_copy, I32, 2 * CW, split)
         for c in range(1, NCH):
             quant(c)
-        project(0, 0)
-        store_half(0, 0)
-        project(0, 1)
-        store_half(0, 1)
-        for c in range(1, NCH):
+        for c in range(NCH):
             project(c, 0)
             project(c, 1)
             store(c)

@@ -1,6 +1,7 @@
 from contextlib import ExitStack
 
 import concourse.mybir as mybir
+from concourse.masks import make_identity
 
 D, T, S, N, NQ = 512, 2048, 1024, 512, 256
 FLOPS = 2 * D * N * NQ
@@ -34,28 +35,28 @@ def tile_attend_pre_edge_f_topk_kernel(tc, qT, kT, rT, ob, offs, offs2, out):
         r_rows = rT.rearrange("(p t) s -> p t s", t=PACK)
         k_rows = kT.rearrange("(p t) s -> p t s", t=PACK)
         q_rows = qT[0].rearrange("(p t) q -> p t q", t=PACK)
-        r_early = keep.tile([P, PACK - 1, S], F32, name="r_early")
-        r_last = keep.tile([P, S], F32, name="r_last")
+        r_tab = [keep.tile([P, 2, S], F32, name=f"r_tab{j}") for j in range(2)]
         k_tab = [keep.tile([P, T], F32, name=f"k_tab{t}") for t in range(PACK)]
         stage = [keep.tile([P, PACK * P], F32, name=f"stage{h}", align_bytes=64) for h in range(2)]
         q_raw = [stage[h][:].rearrange("p (t q) -> p t q", t=PACK) for h in range(2)]
-        bias = [keep.tile([P, 1], F32, name=f"bias{h}") for h in range(2)]
+        biases = keep.tile([P, 2], F32, name="biases")
+        bias = [biases[:, h:h + 1] for h in range(2)]
 
-        nc.sync.dma_start(r_early[:], r_rows[:, 0:PACK - 1, :])
+        nc.sync.dma_start(r_tab[1][:], r_rows[:, 2:4, :])
         nc.sync.dma_start(r_list[:], offs2)
-        nc.sync.dma_start(k_tab[0][:], k_rows[:, 0, :])
+        nc.sync.dma_start(r_tab[0][:], r_rows[:, 0:2, :])
         nc.sync.dma_start(k_list[:], offs)
-        for t in range(1, PACK):
+        for t in (2, 3, 1, 0):
             nc.sync.dma_start(k_tab[t][:], k_rows[:, t, :])
-        nc.sync.dma_start(r_last[:], r_rows[:, PACK - 1, :])
         for h in range(2):
             nc.sync.dma_start(q_raw[h], q_rows[:, :, h * P:(h + 1) * P])
-        for h in range(2):
-            nc.sync.dma_start(bias[h][:], ob[0, h * P:(h + 1) * P, :])
+        with nc.allow_non_contiguous_dma(reason="one bias to a partition for each half of the outputs"):
+            nc.sync.dma_start(biases[:], ob[0].rearrange("(h p) o -> p (h o)", p=P))
 
-        r_g = keep.tile([P, PACK - 1, N], F32, name="r_g")
+        r_g = keep.tile([P, PACK, N], F32, name="r_g")
         k_g = keep.tile([P, PACK, N], F32, name="k_g")
-        r3_g = r_g[:, 2, :]
+        ident = keep.tile([P, P], F32, name="ident")
+        make_identity(nc, ident[:])
         pair_all = keep.tile([P, 2 * N * 2], BF16, name="pair_all")
         first = keep.tile([P, (CW + P) * PACK], BF16, name="first", align_bytes=64)
         q_hi = keep.tile([P, P * PACK], BF16, name="q_hi", align_bytes=64)
@@ -81,18 +82,33 @@ def tile_attend_pre_edge_f_topk_kernel(tc, qT, kT, rT, ob, offs, offs2, out):
         def runs(planes, run):
             return planes.rearrange("p t (c i) -> p c t i", i=run)
 
-        for t in range(PACK - 1):
-            nc.vector.tensor_copy(r_g[:, t, :], r_early[:, t, :].indirect(r_list[:]))
-        for t in range(PACK):
-            nc.vector.tensor_copy(k_g[:, t, :], k_tab[t][:].indirect(k_list[:]))
-        for t in range(2):
-            nc.gpsimd.tensor_tensor(pair_lo[:, CW:, t], k_g[:, t, CW:], r_g[:, t, CW:], ALU.subtract)
-        nc.gpsimd.tensor_tensor(woven(0, 0, 2)[:, :, 0:3, :], runs(k_g[:, 0:3, cols(0)], 2), runs(r_g[:, :, cols(0)], 2), ALU.subtract)
-        nc.gpsimd.tensor_tensor(pair_hi[:, CW:, 0], k_g[:, 2, CW:], r_g[:, 2, CW:], ALU.subtract)
+        def first_chunk_diff(t0, t1):
+            nc.gpsimd.tensor_tensor(woven(0, 0, 2)[:, :, t0:t1, :], runs(k_g[:, t0:t1, cols(0)], 2), runs(r_g[:, t0:t1, cols(0)], 2), ALU.subtract)
 
-        for c in range(NCH):
-            nc.vector.tensor_copy(r3_g[:, cols(c)], r_last[:].indirect(r_list[:, c * (CW // 16):(c + 1) * (CW // 16)]))
-        nc.gpsimd.tensor_tensor(first[:, 0:CW * PACK].rearrange("p (n t) -> p n t", t=PACK)[:, :, 3], k_g[:, 3, cols(0)], r3_g[:, cols(0)], ALU.subtract)
+        def into_psum(t, tag_turned, tag_back):
+            turned = psum.tile([P, N - CW], F32, name=f"turned{t}", tag=tag_turned)
+            held = keep.tile([P, N - CW], F32, name=f"held{t}")
+            back = psum.tile([P, N - CW], F32, name=f"back{t}", tag=tag_back)
+            for c in range(1, NCH):
+                nc.tensor.transpose(turned[:, cols(c - 1)], r_g[:, t, cols(c)], ident[:])
+            nc.scalar.copy(held[:], turned[:])
+            for c in range(1, NCH):
+                nc.tensor.transpose(back[:, cols(c - 1)], held[:, cols(c - 1)], ident[:])
+            return back
+
+        for t in (2, 3, 1, 0):
+            nc.vector.tensor_copy(r_g[:, t, :], r_tab[t // 2][:, t % 2, :].indirect(r_list[:]))
+        r_ps = {1: into_psum(1, "bank2_0", "bank3_0"), 0: into_psum(0, "bank2_1", "bank3_1")}
+        for t in (2, 3, 1):
+            nc.vector.tensor_copy(k_g[:, t, :], k_tab[t][:].indirect(k_list[:]))
+        for t in (2, 3):
+            nc.gpsimd.tensor_tensor(pair_hi[:, CW:, t - 2], k_g[:, t, CW:], r_g[:, t, CW:], ALU.subtract)
+        first_chunk_diff(1, 4)
+        nc.vector.tensor_tensor(pair_lo[:, CW:, 1], k_g[:, 1, CW:], r_ps[1][:], ALU.subtract)
+
+        for j in range(2):
+            nc.vector.tensor_copy(k_g[:, 0, j * HALF:(j + 1) * HALF], k_tab[0][:].indirect(k_list[:, j * (HALF // 16):(j + 1) * (HALF // 16)]))
+        first_chunk_diff(0, 1)
 
         def quant(c):
             nc.vector.quantize_mx(out=codes[c][:].bitcast(FP8X4), scales=scales[c][:], in_=grouped[c])
@@ -102,19 +118,16 @@ def tile_attend_pre_edge_f_topk_kernel(tc, qT, kT, rT, ob, offs, offs2, out):
             nc.tensor.matmul_mx(out=acc[:], lhsT=q_codes[h].bitcast(FP8X4), lhsT_scale=q_scales[h],
                                 rhs=codes[c][:, 0:CW].bitcast(FP8X4), rhs_scale=scales[c][:, 0:CW], start=True, stop=True)
             if c >= 1 and h == 1:
-                nc.vector.tensor_scalar(res[c][:, h, :], acc[:], bias[h][:], 0.0, ALU.add, ALU.max)
+                nc.vector.tensor_scalar(res[c][:, h, :], acc[:], bias[h], 0.0, ALU.add, ALU.max)
             else:
-                nc.scalar.activation(res[c][:, h, :], acc[:], ACT.Relu, bias=bias[h][:])
-
-        def store(c):
-            nc.sync.dma_start(out_v[:, :, cols(c)], res[c][:])
+                nc.scalar.activation(res[c][:, h, :], acc[:], ACT.Relu, bias=bias[h])
 
         def weave_words(copy, dtype, c):
             copy(late[c - 1].bitcast(dtype).rearrange("p (c i u) -> p c u i", i=4, u=2),
                  runs(pair_all[:].bitcast(dtype).rearrange("p (u n) -> p u n", u=2)[:, :, cols(c)], 4))
 
         for c in range(1, NCH):
-            nc.vector.tensor_tensor(pair_hi[:, cols(c), 1], k_g[:, 3, cols(c)], r3_g[:, cols(c)], ALU.subtract)
+            nc.vector.tensor_tensor(pair_lo[:, cols(c), 0], k_g[:, 0, cols(c)], r_ps[0][:, cols(c - 1)], ALU.subtract)
         nc.scalar.copy(woven(0, CW, 4), runs(q_raw[0], 4))
         nc.scalar.copy(woven(NCH, 0, 4), runs(q_raw[1], 4))
         for c in range(1, NCH):
@@ -124,6 +137,9 @@ def tile_attend_pre_edge_f_topk_kernel(tc, qT, kT, rT, ob, offs, offs2, out):
         for c in range(1, NCH):
             quant(c)
         for c in range(NCH):
-            project(c, 0)
-            project(c, 1)
-            store(c)
+            for h in range(2):
+                project(c, h)
+                if c not in (1, 2, 3):
+                    nc.sync.dma_start(out_v[:, h, cols(c)], res[c][:, h, :])
+            if c in (1, 2, 3):
+                nc.sync.dma_start(out_v[:, :, cols(c)], res[c][:])

@@ -39,8 +39,7 @@ def tile_attend_pre_edge_f_topk_kernel(tc, qT, kT, rT, ob, offs, offs2, out):
         k_tab = [keep.tile([P, T], F32, name=f"k_tab{t}") for t in range(PACK)]
         stage = [keep.tile([P, PACK * P], F32, name=f"stage{h}", align_bytes=64) for h in range(2)]
         q_raw = [stage[h][:].rearrange("p (t q) -> p t q", t=PACK) for h in range(2)]
-        biases = keep.tile([P, 2], F32, name="biases")
-        bias = [biases[:, h:h + 1] for h in range(2)]
+        bias = [keep.tile([P, 1], F32, name=f"bias{h}")[:] for h in range(2)]
 
         nc.sync.dma_start(r_tab[1][:], r_rows[:, 2:4, :])
         nc.sync.dma_start(r_list[:], offs2)
@@ -50,8 +49,8 @@ def tile_attend_pre_edge_f_topk_kernel(tc, qT, kT, rT, ob, offs, offs2, out):
             nc.sync.dma_start(k_tab[t][:], k_rows[:, t, :])
         for h in range(2):
             nc.sync.dma_start(q_raw[h], q_rows[:, :, h * P:(h + 1) * P])
-        with nc.allow_non_contiguous_dma(reason="one bias to a partition for each half of the outputs"):
-            nc.sync.dma_start(biases[:], ob[0].rearrange("(h p) o -> p (h o)", p=P))
+        for h in range(2):
+            nc.sync.dma_start(bias[h], ob[0, h * P:(h + 1) * P, :])
 
         r_g = keep.tile([P, PACK, N], F32, name="r_g")
         k_g = keep.tile([P, PACK, N], F32, name="k_g")
@@ -70,7 +69,8 @@ def tile_attend_pre_edge_f_topk_kernel(tc, qT, kT, rT, ob, offs, offs2, out):
         q_scales = [scales[0][:, CW:], scales[NCH][:]]
         pair_lo = pair_all[:, 0:2 * N].rearrange("p (n e) -> p n e", e=2)
         pair_hi = pair_all[:, 2 * N:].rearrange("p (n e) -> p n e", e=2)
-        res = [keep.tile([P, 2, CW], F32, name=f"res{c}") for c in range(NCH)]
+        res_front = keep.tile([P, 2, HALF], F32, name="res_front")
+        res = [res_front[:, :, 0:CW], res_front[:, :, CW:]] + [keep.tile([P, 2, CW], F32, name=f"res{c}")[:] for c in range(2, NCH)]
         out_v = out[0].rearrange("(h p) n -> p h n", p=P)
 
         def cols(c):
@@ -130,16 +130,16 @@ def tile_attend_pre_edge_f_topk_kernel(tc, qT, kT, rT, ob, offs, offs2, out):
             nc.vector.tensor_tensor(pair_lo[:, cols(c), 0], k_g[:, 0, cols(c)], r_ps[0][:, cols(c - 1)], ALU.subtract)
         nc.scalar.copy(woven(0, CW, 4), runs(q_raw[0], 4))
         nc.scalar.copy(woven(NCH, 0, 4), runs(q_raw[1], 4))
-        for c in range(1, NCH):
+        for c in range(2, NCH):
             weave_words(nc.scalar.copy, U32, c)
-        quant(0)
-        quant(NCH)
-        for c in range(1, NCH):
+        weave_words(nc.vector.tensor_copy, I32, 1)
+        for c in (0, 1, NCH, 2, 3):
             quant(c)
-        for c in range(NCH):
-            for h in range(2):
-                project(c, h)
-                if c not in (1, 2, 3):
-                    nc.sync.dma_start(out_v[:, h, cols(c)], res[c][:, h, :])
-            if c in (1, 2, 3):
-                nc.sync.dma_start(out_v[:, :, cols(c)], res[c][:])
+        for h in range(2):
+            project(0, h)
+            project(1, h)
+            nc.sync.dma_start(out_v[:, h, 0:HALF], res_front[:, h, :])
+        for c in range(2, NCH):
+            project(c, 0)
+            project(c, 1)
+            nc.sync.dma_start(out_v[:, :, cols(c)], res[c])

@@ -85,6 +85,10 @@ def tile_attend_pre_edge_f_topk_kernel(tc, qT, kT, rT, ob, offs, offs2, out):
         def first_chunk_diff(t0, t1):
             nc.gpsimd.tensor_tensor(woven(0, 0, 2)[:, :, t0:t1, :], runs(k_g[:, t0:t1, cols(0)], 2), runs(r_g[:, t0:t1, cols(0)], 2), ALU.subtract)
 
+        def gather_halves(t):
+            for j in range(2):
+                nc.vector.tensor_copy(k_g[:, t, j * HALF:(j + 1) * HALF], k_tab[t][:].indirect(k_list[:, j * (HALF // 16):(j + 1) * (HALF // 16)]))
+
         def into_psum(t, tag_turned, tag_back):
             turned = psum.tile([P, N - CW], F32, name=f"turned{t}", tag=tag_turned)
             held = keep.tile([P, N - CW], F32, name=f"held{t}")
@@ -99,15 +103,16 @@ def tile_attend_pre_edge_f_topk_kernel(tc, qT, kT, rT, ob, offs, offs2, out):
         for t in (2, 3, 1, 0):
             nc.vector.tensor_copy(r_g[:, t, :], r_tab[t // 2][:, t % 2, :].indirect(r_list[:]))
         r_ps = {1: into_psum(1, "bank2_0", "bank3_0"), 0: into_psum(0, "bank2_1", "bank3_1")}
-        for t in (2, 3, 1):
+        for t in (2, 3):
             nc.vector.tensor_copy(k_g[:, t, :], k_tab[t][:].indirect(k_list[:]))
+        gather_halves(1)
         for t in (2, 3):
             nc.gpsimd.tensor_tensor(pair_hi[:, CW:, t - 2], k_g[:, t, CW:], r_g[:, t, CW:], ALU.subtract)
         first_chunk_diff(1, 4)
-        nc.vector.tensor_tensor(pair_lo[:, CW:, 1], k_g[:, 1, CW:], r_ps[1][:], ALU.subtract)
+        nc.vector.tensor_tensor(pair_lo[:, cols(1), 1], k_g[:, 1, cols(1)], r_ps[1][:, 0:CW], ALU.subtract)
+        nc.vector.tensor_tensor(pair_lo[:, HALF:, 1], k_g[:, 1, HALF:], r_ps[1][:, CW:], ALU.subtract)
 
-        for j in range(2):
-            nc.vector.tensor_copy(k_g[:, 0, j * HALF:(j + 1) * HALF], k_tab[0][:].indirect(k_list[:, j * (HALF // 16):(j + 1) * (HALF // 16)]))
+        gather_halves(0)
         first_chunk_diff(0, 1)
 
         def quant(c):

@@ -28,6 +28,7 @@ def tile_attend_pre_edge_f_topk_kernel(tc, qT, kT, rT, ob, offs, offs2, out):
     with ExitStack() as ctx:
         lists = ctx.enter_context(tc.tile_pool(name="lists", bufs=1))
         keep = ctx.enter_context(tc.tile_pool(name="keep", bufs=1))
+        moved = ctx.enter_context(tc.tile_pool(name="moved", bufs=1))
         psum = ctx.enter_context(tc.psum_pool(name="psum", bufs=1))
 
         k_list = lists.tile([P, N // 16], U16, name="k_list")
@@ -35,9 +36,9 @@ def tile_attend_pre_edge_f_topk_kernel(tc, qT, kT, rT, ob, offs, offs2, out):
         r_rows = rT.rearrange("(p t) s -> p t s", t=PACK)
         k_rows = kT.rearrange("(p t) s -> p t s", t=PACK)
         q_rows = qT[0].rearrange("(p t) q -> p t q", t=PACK)
-        r_tab = [keep.tile([P, 2, S], F32, name=f"r_tab{j}") for j in range(2)]
-        k_tab = [keep.tile([P, T], F32, name=f"k_tab{t}") for t in range(PACK)]
-        stage = [keep.tile([P, PACK * P], F32, name=f"stage{h}", align_bytes=64) for h in range(2)]
+        r_tab = [moved.tile([P, 2, S], F32, name=f"r_tab{j}", align_bytes=256) for j in range(2)]
+        k_tab = [moved.tile([P, T], F32, name=f"k_tab{t}", align_bytes=256) for t in range(PACK)]
+        stage = [moved.tile([P, PACK * P], F32, name=f"stage{h}", align_bytes=256) for h in range(2)]
         q_raw = [stage[h][:].rearrange("p (t q) -> p t q", t=PACK) for h in range(2)]
         bias = [keep.tile([P, 1], F32, name=f"bias{h}")[:] for h in range(2)]
 
@@ -69,8 +70,8 @@ def tile_attend_pre_edge_f_topk_kernel(tc, qT, kT, rT, ob, offs, offs2, out):
         q_scales = [scales[0][:, CW:], scales[NCH][:]]
         pair_lo = pair_all[:, 0:2 * N].rearrange("p (n e) -> p n e", e=2)
         pair_hi = pair_all[:, 2 * N:].rearrange("p (n e) -> p n e", e=2)
-        res_front = keep.tile([P, 2, HALF], F32, name="res_front")
-        res = [res_front[:, :, 0:CW], res_front[:, :, CW:]] + [keep.tile([P, 2, CW], F32, name=f"res{c}")[:] for c in range(2, NCH)]
+        res_front = moved.tile([P, 2, HALF], F32, name="res_front", align_bytes=256)
+        res = [res_front[:, :, 0:CW], res_front[:, :, CW:]] + [moved.tile([P, 2, CW], F32, name=f"res{c}", align_bytes=256)[:] for c in range(2, NCH)]
         out_v = out[0].rearrange("(h p) n -> p h n", p=P)
 
         def cols(c):

@@ -21,6 +21,7 @@ PACK = 4
 HALF = N // 2
 CW = 128
 NCH = N // CW
+PAIRED = 64
 
 
 def tile_attend_pre_edge_f_topk_kernel(tc, qT, kT, rT, ob, offs, offs2, out):
@@ -38,8 +39,11 @@ def tile_attend_pre_edge_f_topk_kernel(tc, qT, kT, rT, ob, offs, offs2, out):
         q_rows = qT[0].rearrange("(p t) q -> p t q", t=PACK)
         r_tab = [moved.tile([P, 2, S], F32, name=f"r_tab{j}", align_bytes=256) for j in range(2)]
         k_tab = [moved.tile([P, T], F32, name=f"k_tab{t}", align_bytes=256) for t in range(PACK)]
-        stage = [moved.tile([P, PACK * P], F32, name=f"stage{h}", align_bytes=256) for h in range(2)]
-        q_raw = [stage[h][:].rearrange("p (t q) -> p t q", t=PACK) for h in range(2)]
+        words = CW * PACK // 2
+        direct_at = PACK * P
+        front = moved.tile([P, direct_at + (HALF - PAIRED + P) * PACK // 2], F32, name="front", align_bytes=256)
+        back_stage = moved.tile([P, PACK * P], F32, name="back_stage", align_bytes=256)
+        q_raw = [s.rearrange("p (t q) -> p t q", t=PACK) for s in (front[:, 0:direct_at], back_stage[:])]
         bias = [keep.tile([P, 1], F32, name=f"bias{h}")[:] for h in range(2)]
 
         nc.sync.dma_start(r_tab[1][:], r_rows[:, 2:4, :])
@@ -58,11 +62,12 @@ def tile_attend_pre_edge_f_topk_kernel(tc, qT, kT, rT, ob, offs, offs2, out):
         ident = keep.tile([P, P], F32, name="ident")
         make_identity(nc, ident[:])
         pair_all = keep.tile([P, 2 * N * 2], BF16, name="pair_all")
-        first = keep.tile([P, (CW + P) * PACK], BF16, name="first", align_bytes=64)
         q_hi = keep.tile([P, P * PACK], BF16, name="q_hi", align_bytes=64)
-        words = CW * PACK // 2
-        late = [stage[0][:, 0:words], stage[0][:, words:], stage[1][:, 0:words]]
-        grouped = [first[:]] + [w.bitcast(BF16) for w in late] + [q_hi[:]]
+        second_at = direct_at - 2 * PAIRED
+        late = [front[:, second_at:second_at + words], front[:, 0:words], back_stage[:, 0:words]]
+        grouped = [front[:, second_at + words:].bitcast(BF16)] + [w.bitcast(BF16) for w in late] + [q_hi[:]]
+        direct = front[:, direct_at:second_at + 2 * words].bitcast(BF16).rearrange("p (n t) -> p n t", t=PACK)
+        chunk_at = (CW, 0, 2 * CW, 3 * CW)
         widths = [CW + P] + [CW] * NCH
         codes = [keep.tile([P, w], U32, name=f"codes{c}", align_bytes=64) for c, w in enumerate(widths)]
         scales = [keep.tile([P, w], U8, name=f"scales{c}", align_bytes=64) for c, w in enumerate(widths)]
@@ -71,7 +76,7 @@ def tile_attend_pre_edge_f_topk_kernel(tc, qT, kT, rT, ob, offs, offs2, out):
         pair_lo = pair_all[:, 0:2 * N].rearrange("p (n e) -> p n e", e=2)
         pair_hi = pair_all[:, 2 * N:].rearrange("p (n e) -> p n e", e=2)
         res_front = moved.tile([P, 2, HALF], F32, name="res_front", align_bytes=256)
-        res = [res_front[:, :, 0:CW], res_front[:, :, CW:]] + [moved.tile([P, 2, CW], F32, name=f"res{c}", align_bytes=256)[:] for c in range(2, NCH)]
+        res = [res_front[:, :, CW:], res_front[:, :, 0:CW]] + [moved.tile([P, 2, CW], F32, name=f"res{c}", align_bytes=256)[:] for c in range(2, NCH)]
         out_v = out[0].rearrange("(h p) n -> p h n", p=P)
 
         def cols(c):
@@ -83,8 +88,8 @@ def tile_attend_pre_edge_f_topk_kernel(tc, qT, kT, rT, ob, offs, offs2, out):
         def runs(planes, run):
             return planes.rearrange("p t (c i) -> p c t i", i=run)
 
-        def first_chunk_diff(t0, t1):
-            nc.gpsimd.tensor_tensor(woven(0, 0, 2)[:, :, t0:t1, :], runs(k_g[:, t0:t1, cols(0)], 2), runs(r_g[:, t0:t1, cols(0)], 2), ALU.subtract)
+        def direct_diff(t):
+            nc.gpsimd.tensor_tensor(direct[:, :, t], k_g[:, t, PAIRED:HALF], r_g[:, t, PAIRED:HALF], ALU.subtract)
 
         def gather_halves(t):
             for j in range(2):
@@ -95,7 +100,7 @@ def tile_attend_pre_edge_f_topk_kernel(tc, qT, kT, rT, ob, offs, offs2, out):
             held = keep.tile([P, N - CW], F32, name=f"held{t}")
             back = psum.tile([P, N - CW], F32, name=f"back{t}", tag=tag_back)
             for c in range(1, NCH):
-                nc.tensor.transpose(turned[:, cols(c - 1)], r_g[:, t, cols(c)], ident[:])
+                nc.tensor.transpose(turned[:, cols(c - 1)], r_g[:, t, chunk_at[c]:chunk_at[c] + CW], ident[:])
             nc.scalar.copy(held[:], turned[:])
             for c in range(1, NCH):
                 nc.tensor.transpose(back[:, cols(c - 1)], held[:, cols(c - 1)], ident[:])
@@ -108,13 +113,15 @@ def tile_attend_pre_edge_f_topk_kernel(tc, qT, kT, rT, ob, offs, offs2, out):
             nc.vector.tensor_copy(k_g[:, t, :], k_tab[t][:].indirect(k_list[:]))
         gather_halves(1)
         for t in (2, 3):
-            nc.gpsimd.tensor_tensor(pair_hi[:, CW:, t - 2], k_g[:, t, CW:], r_g[:, t, CW:], ALU.subtract)
-        first_chunk_diff(1, 4)
-        nc.vector.tensor_tensor(pair_lo[:, cols(1), 1], k_g[:, 1, cols(1)], r_ps[1][:, 0:CW], ALU.subtract)
+            nc.gpsimd.tensor_tensor(pair_hi[:, HALF:, t - 2], k_g[:, t, HALF:], r_g[:, t, HALF:], ALU.subtract)
+            direct_diff(t)
+        nc.gpsimd.tensor_tensor(pair_hi[:, 0:PAIRED, :].rearrange("p n e -> p e n"), k_g[:, 2:4, 0:PAIRED], r_g[:, 2:4, 0:PAIRED], ALU.subtract)
+        direct_diff(1)
+        nc.vector.tensor_tensor(pair_lo[:, 0:PAIRED, 1], k_g[:, 1, 0:PAIRED], r_ps[1][:, 0:PAIRED], ALU.subtract)
         nc.vector.tensor_tensor(pair_lo[:, HALF:, 1], k_g[:, 1, HALF:], r_ps[1][:, CW:], ALU.subtract)
 
         gather_halves(0)
-        first_chunk_diff(0, 1)
+        direct_diff(0)
 
         def quant(c):
             nc.vector.quantize_mx(out=codes[c][:].bitcast(FP8X4), scales=scales[c][:], in_=grouped[c])
@@ -128,17 +135,18 @@ def tile_attend_pre_edge_f_topk_kernel(tc, qT, kT, rT, ob, offs, offs2, out):
             else:
                 nc.scalar.activation(res[c][:, h, :], acc[:], ACT.Relu, bias=bias[h])
 
-        def weave_words(copy, dtype, c):
-            copy(late[c - 1].bitcast(dtype).rearrange("p (c i u) -> p c u i", i=4, u=2),
-                 runs(pair_all[:].bitcast(dtype).rearrange("p (u n) -> p u n", u=2)[:, :, cols(c)], 4))
+        def weave_words(copy, dtype, c, count):
+            copy(late[c - 1][:, 0:2 * count].bitcast(dtype).rearrange("p (c i u) -> p c u i", i=4, u=2),
+                 runs(pair_all[:].bitcast(dtype).rearrange("p (u n) -> p u n", u=2)[:, :, chunk_at[c]:chunk_at[c] + count], 4))
 
-        for c in range(1, NCH):
+        nc.vector.tensor_tensor(pair_lo[:, 0:PAIRED, 0], k_g[:, 0, 0:PAIRED], r_ps[0][:, 0:PAIRED], ALU.subtract)
+        for c in range(2, NCH):
             nc.vector.tensor_tensor(pair_lo[:, cols(c), 0], k_g[:, 0, cols(c)], r_ps[0][:, cols(c - 1)], ALU.subtract)
         nc.scalar.copy(woven(0, CW, 4), runs(q_raw[0], 4))
         nc.scalar.copy(woven(NCH, 0, 4), runs(q_raw[1], 4))
         for c in range(2, NCH):
-            weave_words(nc.scalar.copy, U32, c)
-        weave_words(nc.vector.tensor_copy, I32, 1)
+            weave_words(nc.scalar.copy, U32, c, CW)
+        weave_words(nc.vector.tensor_copy, I32, 1, PAIRED)
         for c in (0, 1, NCH, 2, 3):
             quant(c)
         for h in range(2):

@@ -69,10 +69,11 @@ def tile_attend_pre_edge_f_topk_kernel(tc, qT, kT, rT, ob, offs, offs2, out):
         direct = front[:, direct_at:second_at + 2 * words].bitcast(BF16).rearrange("p (n t) -> p n t", t=PACK)
         chunk_at = (CW, 0, 2 * CW, 3 * CW)
         widths = [CW + P] + [CW] * NCH
-        codes = [keep.tile([P, w], U32, name=f"codes{c}", align_bytes=64) for c, w in enumerate(widths)]
-        scales = [keep.tile([P, w], U8, name=f"scales{c}", align_bytes=64) for c, w in enumerate(widths)]
+        starts = [64] * NCH + [192]
+        codes = [keep.tile([P, w], U32, name=f"codes{c}", align_bytes=256) for c, w in enumerate(widths)]
+        scales = [keep.tile([P, s + w], U8, name=f"scales{c}", align_bytes=256)[:, s:] for c, (w, s) in enumerate(zip(widths, starts))]
         q_codes = [codes[0][:, CW:], codes[NCH][:]]
-        q_scales = [scales[0][:, CW:], scales[NCH][:]]
+        q_scales = [scales[0][:, CW:], scales[NCH]]
         pair_lo = pair_all[:, 0:2 * N].rearrange("p (n e) -> p n e", e=2)
         pair_hi = pair_all[:, 2 * N:].rearrange("p (n e) -> p n e", e=2)
         res_front = moved.tile([P, 2, HALF], F32, name="res_front", align_bytes=256)
@@ -124,7 +125,7 @@ def tile_attend_pre_edge_f_topk_kernel(tc, qT, kT, rT, ob, offs, offs2, out):
         direct_diff(0)
 
         def quant(c):
-            nc.vector.quantize_mx(out=codes[c][:].bitcast(FP8X4), scales=scales[c][:], in_=grouped[c])
+            nc.vector.quantize_mx(out=codes[c][:].bitcast(FP8X4), scales=scales[c], in_=grouped[c])
 
         def project(c, h):
             acc = psum.tile([P, CW], F32, name=f"acc{c}_{h}", tag=f"bank{c}_{h}")

@@ -9,7 +9,6 @@ FLOPS = 2 * D * N * NQ
 F32 = mybir.dt.float32
 BF16 = mybir.dt.bfloat16
 U32 = mybir.dt.uint32
-I32 = mybir.dt.int32
 U16 = mybir.dt.uint16
 U8 = mybir.dt.uint8
 FP8X4 = mybir.dt.float8_e4m3fn_x4
@@ -21,7 +20,8 @@ PACK = 4
 HALF = N // 2
 CW = 128
 NCH = N // CW
-PAIRED = 64
+LEAD = 64
+POOL_END = HALF + 160
 
 
 def tile_attend_pre_edge_f_topk_kernel(tc, qT, kT, rT, ob, offs, offs2, out):
@@ -29,7 +29,6 @@ def tile_attend_pre_edge_f_topk_kernel(tc, qT, kT, rT, ob, offs, offs2, out):
     with ExitStack() as ctx:
         lists = ctx.enter_context(tc.tile_pool(name="lists", bufs=1))
         keep = ctx.enter_context(tc.tile_pool(name="keep", bufs=1))
-        moved = ctx.enter_context(tc.tile_pool(name="moved", bufs=1))
         psum = ctx.enter_context(tc.psum_pool(name="psum", bufs=1))
 
         k_list = lists.tile([P, N // 16], U16, name="k_list")
@@ -37,124 +36,120 @@ def tile_attend_pre_edge_f_topk_kernel(tc, qT, kT, rT, ob, offs, offs2, out):
         r_rows = rT.rearrange("(p t) s -> p t s", t=PACK)
         k_rows = kT.rearrange("(p t) s -> p t s", t=PACK)
         q_rows = qT[0].rearrange("(p t) q -> p t q", t=PACK)
-        r_tab = [moved.tile([P, 2, S], F32, name=f"r_tab{j}", align_bytes=256) for j in range(2)]
-        k_tab = [moved.tile([P, T], F32, name=f"k_tab{t}", align_bytes=256) for t in range(PACK)]
-        words = CW * PACK // 2
-        direct_at = PACK * P
-        front = moved.tile([P, direct_at + (HALF - PAIRED + P) * PACK // 2], F32, name="front", align_bytes=256)
-        back_stage = moved.tile([P, PACK * P], F32, name="back_stage", align_bytes=256)
-        q_raw = [s.rearrange("p (t q) -> p t q", t=PACK) for s in (front[:, 0:direct_at], back_stage[:])]
-        bias = [keep.tile([P, 1], F32, name=f"bias{h}")[:] for h in range(2)]
+        r_tab = [keep.tile([P, 2, S], F32, name=f"r_tab{j}", align_bytes=256) for j in range(2)]
+        k_tab = [keep.tile([P, T], F32, name=f"k_tab{t}", align_bytes=256) for t in range(PACK)]
+        q_raw = [keep.tile([P, PACK, P], F32, name=f"q_raw{h}", align_bytes=256) for h in range(2)]
+        bias_rows = keep.tile([P, P], F32, name="bias_rows", align_bytes=256)
+        nc.vector.memset(bias_rows[:], 0.0)
 
         nc.sync.dma_start(r_tab[1][:], r_rows[:, 2:4, :])
         nc.sync.dma_start(r_list[:], offs2)
         nc.sync.dma_start(r_tab[0][:], r_rows[:, 0:2, :])
         nc.sync.dma_start(k_list[:], offs)
-        for t in (2, 3, 1, 0):
+        nc.sync.dma_start(bias_rows[0:2, :], ob[0].rearrange("(h p) o -> h (p o)", h=2))
+        for t in (3, 2, 1, 0):
             nc.sync.dma_start(k_tab[t][:], k_rows[:, t, :])
         for h in range(2):
-            nc.sync.dma_start(q_raw[h], q_rows[:, :, h * P:(h + 1) * P])
-        for h in range(2):
-            nc.sync.dma_start(bias[h], ob[0, h * P:(h + 1) * P, :])
+            nc.sync.dma_start(q_raw[h][:], q_rows[:, :, h * P:(h + 1) * P])
 
-        r_g = keep.tile([P, PACK, N], F32, name="r_g")
-        k_g = keep.tile([P, PACK, N], F32, name="k_g")
         ident = keep.tile([P, P], F32, name="ident")
         make_identity(nc, ident[:])
-        pair_all = keep.tile([P, 2 * N * 2], BF16, name="pair_all")
-        q_hi = keep.tile([P, P * PACK], BF16, name="q_hi", align_bytes=64)
-        second_at = direct_at - 2 * PAIRED
-        late = [front[:, second_at:second_at + words], front[:, 0:words], back_stage[:, 0:words]]
-        grouped = [front[:, second_at + words:].bitcast(BF16)] + [w.bitcast(BF16) for w in late] + [q_hi[:]]
-        direct = front[:, direct_at:second_at + 2 * words].bitcast(BF16).rearrange("p (n t) -> p n t", t=PACK)
-        chunk_at = (CW, 0, 2 * CW, 3 * CW)
-        widths = [CW + P] + [CW] * NCH
-        starts = [64] * NCH + [192]
-        codes = [keep.tile([P, w], U32, name=f"codes{c}", align_bytes=256) for c, w in enumerate(widths)]
-        scales = [keep.tile([P, s + w], U8, name=f"scales{c}", align_bytes=256)[:, s:] for c, (w, s) in enumerate(zip(widths, starts))]
-        q_codes = [codes[0][:, CW:], codes[NCH][:]]
-        q_scales = [scales[0][:, CW:], scales[NCH]]
-        pair_lo = pair_all[:, 0:2 * N].rearrange("p (n e) -> p n e", e=2)
-        pair_hi = pair_all[:, 2 * N:].rearrange("p (n e) -> p n e", e=2)
-        res_front = moved.tile([P, 2, HALF], F32, name="res_front", align_bytes=256)
-        res = [res_front[:, :, CW:], res_front[:, :, 0:CW]] + [moved.tile([P, 2, CW], F32, name=f"res{c}", align_bytes=256)[:] for c in range(2, NCH)]
-        out_v = out[0].rearrange("(h p) n -> p h n", p=P)
+        r_g = keep.tile([P, PACK, N], F32, name="r_g")
+        k_g = keep.tile([P, PACK, N], F32, name="k_g")
+        u = keep.tile([P, N * PACK], BF16, name="u", align_bytes=64)
+        u_v = u[:].rearrange("p (n t) -> p n t", t=PACK)
+        q_bf = [keep.tile([P, P * PACK], BF16, name=f"q_bf{h}", align_bytes=64) for h in range(2)]
+        u_codes = [keep.tile([P, CW], U32, name=f"u_codes{c}", align_bytes=256) for c in range(NCH)]
+        u_scales = [keep.tile([P, 64 + CW], U8, name=f"u_scales{c}", align_bytes=256)[:, 64:] for c in range(NCH)]
+        q_codes = [keep.tile([P, P], U32, name=f"q_codes{h}", align_bytes=256) for h in range(2)]
+        q_scales = [keep.tile([P, 192 + P], U8, name=f"q_scales{h}", align_bytes=256)[:, 192:] for h in range(2)]
+        res = [[keep.tile([P, HALF], F32, name=f"res{h}_{j}", align_bytes=256) for j in range(2)] for h in range(2)]
+        bias = keep.tile([P, 2], F32, name="bias")
 
         def cols(c):
             return slice(c * CW, (c + 1) * CW)
 
-        def woven(c, first, run):
-            return grouped[c][:, first * PACK:(first + CW) * PACK].rearrange("p (c i t) -> p c t i", i=run, t=PACK)
+        def entries(first, last):
+            return k_list[:, first // 16:last // 16]
 
-        def runs(planes, run):
-            return planes.rearrange("p t (c i) -> p c t i", i=run)
+        bias_ps = psum.tile([P, P], F32, name="bias_ps", tag="bank2")
+        nc.tensor.transpose(bias_ps[:], bias_rows[:], ident[:])
+        nc.scalar.copy(bias[:], bias_ps[:, 0:2])
 
-        def direct_diff(t):
-            nc.gpsimd.tensor_tensor(direct[:, :, t], k_g[:, t, PAIRED:HALF], r_g[:, t, PAIRED:HALF], ALU.subtract)
+        blocks = (0, 1, 3)
 
-        def gather_halves(t):
-            for j in range(2):
-                nc.vector.tensor_copy(k_g[:, t, j * HALF:(j + 1) * HALF], k_tab[t][:].indirect(k_list[:, j * (HALF // 16):(j + 1) * (HALF // 16)]))
-
-        def into_psum(t, tag_turned, tag_back):
-            turned = psum.tile([P, N - CW], F32, name=f"turned{t}", tag=tag_turned)
-            held = keep.tile([P, N - CW], F32, name=f"held{t}")
-            back = psum.tile([P, N - CW], F32, name=f"back{t}", tag=tag_back)
-            for c in range(1, NCH):
-                nc.tensor.transpose(turned[:, cols(c - 1)], r_g[:, t, chunk_at[c]:chunk_at[c] + CW], ident[:])
+        def into_psum(name, parts, tag_turned, tag_back):
+            turned = psum.tile([P, 3 * CW], F32, name=f"turned_{name}", tag=tag_turned)
+            held = keep.tile([P, 3 * CW], F32, name=f"held_{name}")
+            back = psum.tile([P, 3 * CW], F32, name=f"back_{name}", tag=tag_back)
+            for b, part in enumerate(parts):
+                nc.tensor.transpose(turned[:, cols(b)], part, ident[:])
             nc.scalar.copy(held[:], turned[:])
-            for c in range(1, NCH):
-                nc.tensor.transpose(back[:, cols(c - 1)], held[:, cols(c - 1)], ident[:])
-            return back
+            for b in range(3):
+                nc.tensor.transpose(back[:, cols(b)], held[:, cols(b)], ident[:])
+            return back[:].rearrange("p (b n) -> p b n", b=3)
 
-        for t in (2, 3, 1, 0):
+        for t in (3, 2, 1, 0):
             nc.vector.tensor_copy(r_g[:, t, :], r_tab[t // 2][:, t % 2, :].indirect(r_list[:]))
-        r_ps = {1: into_psum(1, "bank2_0", "bank3_0"), 0: into_psum(0, "bank2_1", "bank3_1")}
-        for t in (2, 3):
-            nc.vector.tensor_copy(k_g[:, t, :], k_tab[t][:].indirect(k_list[:]))
-        gather_halves(1)
-        for t in (2, 3):
-            nc.gpsimd.tensor_tensor(pair_hi[:, HALF:, t - 2], k_g[:, t, HALF:], r_g[:, t, HALF:], ALU.subtract)
-            direct_diff(t)
-        nc.gpsimd.tensor_tensor(pair_hi[:, 0:PAIRED, :].rearrange("p n e -> p e n"), k_g[:, 2:4, 0:PAIRED], r_g[:, 2:4, 0:PAIRED], ALU.subtract)
-        direct_diff(1)
-        nc.vector.tensor_tensor(pair_lo[:, 0:PAIRED, 1], k_g[:, 1, 0:PAIRED], r_ps[1][:, 0:PAIRED], ALU.subtract)
-        nc.vector.tensor_tensor(pair_lo[:, HALF:, 1], k_g[:, 1, HALF:], r_ps[1][:, CW:], ALU.subtract)
+        r_top = into_psum("top", [r_g[:, 3, cols(c)] for c in blocks], "bank0", "bank4")
+        r_low = {c: into_psum(f"low{c}", [r_g[:, t, cols(c)] for t in range(3)], f"bank{(b + 1) % 2}", f"bank{5 + b}") for b, c in enumerate(blocks)}
 
-        gather_halves(0)
-        direct_diff(0)
+        def gather_v(t, first, last):
+            nc.vector.tensor_copy(k_g[:, t, first:last], k_tab[t][:].indirect(entries(first, last)))
 
-        def quant(c):
-            nc.vector.quantize_mx(out=codes[c][:].bitcast(FP8X4), scales=scales[c], in_=grouped[c])
+        def gather_s(t, first, last):
+            nc.scalar.activation(k_g[:, t, first:last], k_tab[t][:].indirect(entries(first, last)), ACT.Copy)
 
-        def project(c, h):
-            acc = psum.tile([P, CW], F32, name=f"acc{c}_{h}", tag=f"bank{c}_{h}")
-            nc.tensor.matmul_mx(out=acc[:], lhsT=q_codes[h].bitcast(FP8X4), lhsT_scale=q_scales[h],
-                                rhs=codes[c][:, 0:CW].bitcast(FP8X4), rhs_scale=scales[c][:, 0:CW], start=True, stop=True)
-            if c >= 1 and h == 1:
-                nc.vector.tensor_scalar(res[c][:, h, :], acc[:], bias[h], 0.0, ALU.add, ALU.max)
-            else:
-                nc.scalar.activation(res[c][:, h, :], acc[:], ACT.Relu, bias=bias[h])
+        def diff_low(first, last):
+            c = first // CW
+            nc.vector.tensor_tensor(u_v[:, first:last, 0:3], k_g[:, 0:3, first:last].rearrange("p t n -> p n t"),
+                                    r_low[c][:, :, first - c * CW:last - c * CW].rearrange("p t n -> p n t"), ALU.subtract)
 
-        def weave_words(copy, dtype, c, count):
-            copy(late[c - 1][:, 0:2 * count].bitcast(dtype).rearrange("p (c i u) -> p c u i", i=4, u=2),
-                 runs(pair_all[:].bitcast(dtype).rearrange("p (u n) -> p u n", u=2)[:, :, chunk_at[c]:chunk_at[c] + count], 4))
+        def diff_g(t, first, last):
+            nc.gpsimd.tensor_tensor(u_v[:, first:last, t], k_g[:, t, first:last], r_g[:, t, first:last], ALU.subtract)
 
-        nc.vector.tensor_tensor(pair_lo[:, 0:PAIRED, 0], k_g[:, 0, 0:PAIRED], r_ps[0][:, 0:PAIRED], ALU.subtract)
-        for c in range(2, NCH):
-            nc.vector.tensor_tensor(pair_lo[:, cols(c), 0], k_g[:, 0, cols(c)], r_ps[0][:, cols(c - 1)], ALU.subtract)
-        nc.scalar.copy(woven(0, CW, 4), runs(q_raw[0], 4))
-        nc.scalar.copy(woven(NCH, 0, 4), runs(q_raw[1], 4))
-        for c in range(2, NCH):
-            weave_words(nc.scalar.copy, U32, c, CW)
-        weave_words(nc.vector.tensor_copy, I32, 1, PAIRED)
-        for c in (0, 1, NCH, 2, 3):
-            quant(c)
+        for t in (3, 2, 1):
+            gather_v(t, 0, HALF)
+            gather_s(t, HALF, N)
+            diff_g(t, HALF, POOL_END)
+        r_top_flat = r_top.rearrange("p b n -> p (b n)")
+        nc.vector.tensor_tensor(u_v[:, 0:HALF, 3], k_g[:, 3, 0:HALF], r_top_flat[:, 0:HALF], ALU.subtract)
+        nc.vector.tensor_tensor(u_v[:, POOL_END:N, 3], k_g[:, 3, POOL_END:N], r_top_flat[:, POOL_END - CW:], ALU.subtract)
+        gather_s(0, 0, LEAD)
+        gather_s(0, HALF, POOL_END)
+        gather_s(0, POOL_END, N)
+        gather_v(0, LEAD, HALF)
+        diff_g(0, HALF, POOL_END)
+        diff_low(0, LEAD)
+        diff_low(LEAD, CW)
+        diff_low(CW, HALF)
+        diff_low(POOL_END, N)
+
         for h in range(2):
-            project(0, h)
-            project(1, h)
-            nc.sync.dma_start(out_v[:, h, 0:HALF], res_front[:, h, :])
-        for c in range(2, NCH):
-            project(c, 0)
-            project(c, 1)
-            nc.sync.dma_start(out_v[:, :, cols(c)], res[c])
+            nc.scalar.copy(q_bf[h][:].rearrange("p (c i t) -> p c t i", i=4, t=PACK), q_raw[h][:].rearrange("p t (c i) -> p c t i", i=4))
+
+        def quant_u(c):
+            woven = u[:, c * CW * PACK:(c + 1) * CW * PACK]
+            nc.vector.quantize_mx(out=u_codes[c][:].bitcast(FP8X4), scales=u_scales[c], in_=woven)
+
+        def quant_q(h):
+            nc.vector.quantize_mx(out=q_codes[h][:].bitcast(FP8X4), scales=q_scales[h], in_=q_bf[h][:])
+
+        quant_u(0)
+        quant_q(0)
+        for c in range(1, NCH):
+            quant_u(c)
+        quant_q(1)
+
+        for h in range(2):
+            for c in range(NCH):
+                acc = psum.tile([P, CW], F32, name=f"acc{h}_{c}", tag=f"bank{NCH * h + c}")
+                nc.tensor.matmul_mx(out=acc[:], lhsT=q_codes[h][:].bitcast(FP8X4), lhsT_scale=q_scales[h],
+                                    rhs=u_codes[c][:].bitcast(FP8X4), rhs_scale=u_scales[c], start=True, stop=True)
+                dst = res[h][c // 2][:, cols(c % 2)]
+                if h == 1 and c % 2 == 0:
+                    nc.vector.tensor_scalar(dst, acc[:], bias[:, h:h + 1], 0.0, ALU.add, ALU.max)
+                else:
+                    nc.scalar.activation(dst, acc[:], ACT.Relu, bias=bias[:, h:h + 1])
+                if c % 2 == 1:
+                    nc.sync.dma_start(out[0, h * P:(h + 1) * P, (c // 2) * HALF:(c // 2 + 1) * HALF], res[h][c // 2][:])

@@ -21,7 +21,8 @@ HALF = N // 2
 CW = 128
 NCH = N // CW
 LEAD = 64
-POOL_END = HALF + 160
+LAST_AT = HALF + 96
+POOL_AT = LAST_AT + 16
 
 
 def tile_attend_pre_edge_f_topk_kernel(tc, qT, kT, rT, ob, offs, offs2, out):
@@ -76,7 +77,7 @@ def tile_attend_pre_edge_f_topk_kernel(tc, qT, kT, rT, ob, offs, offs2, out):
         nc.tensor.transpose(bias_ps[:], bias_rows[:], ident[:])
         nc.scalar.copy(bias[:], bias_ps[:, 0:2])
 
-        blocks = (0, 1, 3)
+        blocks = (0, 1, 2)
 
         def into_psum(name, parts, tag_turned, tag_back):
             turned = psum.tile([P, 3 * CW], F32, name=f"turned_{name}", tag=tag_turned)
@@ -102,8 +103,9 @@ def tile_attend_pre_edge_f_topk_kernel(tc, qT, kT, rT, ob, offs, offs2, out):
 
         def diff_low(first, last):
             c = first // CW
-            nc.vector.tensor_tensor(u_v[:, first:last, 0:3], k_g[:, 0:3, first:last].rearrange("p t n -> p n t"),
-                                    r_low[c][:, :, first - c * CW:last - c * CW].rearrange("p t n -> p n t"), ALU.subtract)
+            nc.vector.tensor_tensor(u_v[:, first:last, 0:3].rearrange("p (c i) t -> p c t i", i=2),
+                                    k_g[:, 0:3, first:last].rearrange("p t (c i) -> p c t i", i=2),
+                                    r_low[c][:, :, first - c * CW:last - c * CW].rearrange("p t (c i) -> p c t i", i=2), ALU.subtract)
 
         def diff_g(t, first, last):
             nc.gpsimd.tensor_tensor(u_v[:, first:last, t], k_g[:, t, first:last], r_g[:, t, first:last], ALU.subtract)
@@ -111,19 +113,17 @@ def tile_attend_pre_edge_f_topk_kernel(tc, qT, kT, rT, ob, offs, offs2, out):
         for t in (3, 2, 1):
             gather_v(t, 0, HALF)
             gather_s(t, HALF, N)
-            diff_g(t, HALF, POOL_END)
-        r_top_flat = r_top.rearrange("p b n -> p (b n)")
-        nc.vector.tensor_tensor(u_v[:, 0:HALF, 3], k_g[:, 3, 0:HALF], r_top_flat[:, 0:HALF], ALU.subtract)
-        nc.vector.tensor_tensor(u_v[:, POOL_END:N, 3], k_g[:, 3, POOL_END:N], r_top_flat[:, POOL_END - CW:], ALU.subtract)
+            diff_g(t, POOL_AT, N)
+        nc.vector.tensor_tensor(u_v[:, 0:POOL_AT, 3], k_g[:, 3, 0:POOL_AT], r_top.rearrange("p b n -> p (b n)")[:, 0:POOL_AT], ALU.subtract)
         gather_s(0, 0, LEAD)
-        gather_s(0, HALF, POOL_END)
-        gather_s(0, POOL_END, N)
+        gather_s(0, LAST_AT, N)
+        gather_s(0, HALF, LAST_AT)
         gather_v(0, LEAD, HALF)
-        diff_g(0, HALF, POOL_END)
+        diff_g(0, POOL_AT, N)
         diff_low(0, LEAD)
         diff_low(LEAD, CW)
         diff_low(CW, HALF)
-        diff_low(POOL_END, N)
+        diff_low(HALF, POOL_AT)
 
         for h in range(2):
             nc.scalar.copy(q_bf[h][:].rearrange("p (c i t) -> p c t i", i=4, t=PACK), q_raw[h][:].rearrange("p t (c i) -> p c t i", i=4))

@@ -40,18 +40,18 @@ def tile_attend_pre_edge_f_topk_kernel(tc, qT, kT, rT, ob, offs, offs2, out):
         r_tab = [keep.tile([P, 2, S], F32, name=f"r_tab{j}", align_bytes=256) for j in range(2)]
         k_tab = [keep.tile([P, T], F32, name=f"k_tab{t}", align_bytes=256) for t in range(PACK)]
         q_raw = [keep.tile([P, PACK, P], F32, name=f"q_raw{h}", align_bytes=256) for h in range(2)]
-        bias_rows = keep.tile([P, P], F32, name="bias_rows", align_bytes=256)
-        nc.vector.memset(bias_rows[:], 0.0)
+        bias = [keep.tile([P, 1], F32, name=f"bias{h}") for h in range(2)]
 
         nc.sync.dma_start(r_tab[1][:], r_rows[:, 2:4, :])
         nc.sync.dma_start(r_list[:], offs2)
         nc.sync.dma_start(r_tab[0][:], r_rows[:, 0:2, :])
         nc.sync.dma_start(k_list[:], offs)
-        nc.sync.dma_start(bias_rows[0:2, :], ob[0].rearrange("(h p) o -> h (p o)", h=2))
         for t in (3, 2, 1, 0):
             nc.sync.dma_start(k_tab[t][:], k_rows[:, t, :])
         for h in range(2):
             nc.sync.dma_start(q_raw[h][:], q_rows[:, :, h * P:(h + 1) * P])
+        for h in range(2):
+            nc.sync.dma_start(bias[h][:], ob[0, h * P:(h + 1) * P, :])
 
         ident = keep.tile([P, P], F32, name="ident")
         make_identity(nc, ident[:])
@@ -65,17 +65,12 @@ def tile_attend_pre_edge_f_topk_kernel(tc, qT, kT, rT, ob, offs, offs2, out):
         q_codes = [keep.tile([P, P], U32, name=f"q_codes{h}", align_bytes=256) for h in range(2)]
         q_scales = [keep.tile([P, 192 + P], U8, name=f"q_scales{h}", align_bytes=256)[:, 192:] for h in range(2)]
         res = [[keep.tile([P, HALF], F32, name=f"res{h}_{j}", align_bytes=256) for j in range(2)] for h in range(2)]
-        bias = keep.tile([P, 2], F32, name="bias")
 
         def cols(c):
             return slice(c * CW, (c + 1) * CW)
 
         def entries(first, last):
             return k_list[:, first // 16:last // 16]
-
-        bias_ps = psum.tile([P, P], F32, name="bias_ps", tag="bank2")
-        nc.tensor.transpose(bias_ps[:], bias_rows[:], ident[:])
-        nc.scalar.copy(bias[:], bias_ps[:, 0:2])
 
         blocks = (0, 1, 2)
 
@@ -92,8 +87,8 @@ def tile_attend_pre_edge_f_topk_kernel(tc, qT, kT, rT, ob, offs, offs2, out):
 
         for t in (3, 2, 1, 0):
             nc.vector.tensor_copy(r_g[:, t, :], r_tab[t // 2][:, t % 2, :].indirect(r_list[:]))
-        r_top = into_psum("top", [r_g[:, 3, cols(c)] for c in blocks], "bank0", "bank4")
-        r_low = {c: into_psum(f"low{c}", [r_g[:, t, cols(c)] for t in range(3)], f"bank{(b + 1) % 2}", f"bank{5 + b}") for b, c in enumerate(blocks)}
+        r_top = into_psum("top", [r_g[:, 3, cols(c)] for c in blocks], "bank3", "bank4")
+        r_low = {c: into_psum(f"low{c}", [r_g[:, t, cols(c)] for t in range(3)], f"bank{b}", f"bank{5 + b}") for b, c in enumerate(blocks)}
 
         def gather_v(t, first, last):
             nc.vector.tensor_copy(k_g[:, t, first:last], k_tab[t][:].indirect(entries(first, last)))
@@ -148,8 +143,8 @@ def tile_attend_pre_edge_f_topk_kernel(tc, qT, kT, rT, ob, offs, offs2, out):
                                     rhs=u_codes[c][:].bitcast(FP8X4), rhs_scale=u_scales[c], start=True, stop=True)
                 dst = res[h][c // 2][:, cols(c % 2)]
                 if h == 1 and c % 2 == 0:
-                    nc.vector.tensor_scalar(dst, acc[:], bias[:, h:h + 1], 0.0, ALU.add, ALU.max)
+                    nc.vector.tensor_scalar(dst, acc[:], bias[h][:], 0.0, ALU.add, ALU.max)
                 else:
-                    nc.scalar.activation(dst, acc[:], ACT.Relu, bias=bias[:, h:h + 1])
+                    nc.scalar.activation(dst, acc[:], ACT.Relu, bias=bias[h][:])
                 if c % 2 == 1:
                     nc.sync.dma_start(out[0, h * P:(h + 1) * P, (c // 2) * HALF:(c // 2 + 1) * HALF], res[h][c // 2][:])

@@ -20,9 +20,7 @@ PACK = 4
 HALF = N // 2
 CW = 128
 NCH = N // CW
-LEAD = 64
-LAST_AT = HALF + 96
-POOL_AT = LAST_AT + 16
+POOL_AT = HALF + 64
 
 
 def tile_attend_pre_edge_f_topk_kernel(tc, qT, kT, rT, ob, offs, offs2, out):
@@ -30,6 +28,7 @@ def tile_attend_pre_edge_f_topk_kernel(tc, qT, kT, rT, ob, offs, offs2, out):
     with ExitStack() as ctx:
         lists = ctx.enter_context(tc.tile_pool(name="lists", bufs=1))
         keep = ctx.enter_context(tc.tile_pool(name="keep", bufs=1))
+        reuse = ctx.enter_context(tc.tile_pool(name="reuse", bufs=1))
         psum = ctx.enter_context(tc.psum_pool(name="psum", bufs=1))
 
         k_list = lists.tile([P, N // 16], U16, name="k_list")
@@ -59,8 +58,9 @@ def tile_attend_pre_edge_f_topk_kernel(tc, qT, kT, rT, ob, offs, offs2, out):
         k_g = keep.tile([P, PACK, N], F32, name="k_g")
         u = keep.tile([P, N * PACK], BF16, name="u", align_bytes=64)
         u_v = u[:].rearrange("p (n t) -> p n t", t=PACK)
-        q_bf = [keep.tile([P, P * PACK], BF16, name=f"q_bf{h}", align_bytes=64) for h in range(2)]
-        u_codes = [keep.tile([P, CW], U32, name=f"u_codes{c}", align_bytes=256) for c in range(NCH)]
+        q_bf = [reuse.tile([P, P * PACK], BF16, name="q_bf0", align_bytes=256, offset=0), keep.tile([P, P * PACK], BF16, name="q_bf1", align_bytes=64)]
+        u_codes = [keep.tile([P, CW], U32, name=f"u_codes{c}", align_bytes=256) for c in range(2)]
+        u_codes = u_codes + [reuse.tile([P, CW], U32, name=f"u_codes{c}", align_bytes=256, offset=4 * CW * (c - 2)) for c in range(2, NCH)]
         u_scales = [keep.tile([P, 64 + CW], U8, name=f"u_scales{c}", align_bytes=256)[:, 64:] for c in range(NCH)]
         q_codes = [keep.tile([P, P], U32, name=f"q_codes{h}", align_bytes=256) for h in range(2)]
         q_scales = [keep.tile([P, 192 + P], U8, name=f"q_scales{h}", align_bytes=256)[:, 192:] for h in range(2)]
@@ -110,15 +110,14 @@ def tile_attend_pre_edge_f_topk_kernel(tc, qT, kT, rT, ob, offs, offs2, out):
             gather_s(t, HALF, N)
             diff_g(t, POOL_AT, N)
         nc.vector.tensor_tensor(u_v[:, 0:POOL_AT, 3], k_g[:, 3, 0:POOL_AT], r_top.rearrange("p b n -> p (b n)")[:, 0:POOL_AT], ALU.subtract)
-        gather_s(0, 0, LEAD)
-        gather_s(0, LAST_AT, N)
-        gather_s(0, HALF, LAST_AT)
-        gather_v(0, LEAD, HALF)
+        gather_s(0, POOL_AT, N)
+        gather_s(0, HALF, POOL_AT)
+        gather_v(0, 0, CW)
+        gather_v(0, CW, HALF)
         diff_g(0, POOL_AT, N)
-        diff_low(0, LEAD)
-        diff_low(LEAD, CW)
-        diff_low(CW, HALF)
+        diff_low(0, CW)
         diff_low(HALF, POOL_AT)
+        diff_low(CW, HALF)
 
         for h in range(2):
             nc.scalar.copy(q_bf[h][:].rearrange("p (c i t) -> p c t i", i=4, t=PACK), q_raw[h][:].rearrange("p t (c i) -> p c t i", i=4))

@@ -28,7 +28,6 @@ def tile_attend_pre_edge_f_topk_kernel(tc, qT, kT, rT, ob, offs, offs2, out):
     with ExitStack() as ctx:
         lists = ctx.enter_context(tc.tile_pool(name="lists", bufs=1))
         keep = ctx.enter_context(tc.tile_pool(name="keep", bufs=1))
-        reuse = ctx.enter_context(tc.tile_pool(name="reuse", bufs=1))
         psum = ctx.enter_context(tc.psum_pool(name="psum", bufs=1))
 
         k_list = lists.tile([P, N // 16], U16, name="k_list")
@@ -58,9 +57,8 @@ def tile_attend_pre_edge_f_topk_kernel(tc, qT, kT, rT, ob, offs, offs2, out):
         k_g = keep.tile([P, PACK, N], F32, name="k_g")
         u = keep.tile([P, N * PACK], BF16, name="u", align_bytes=64)
         u_v = u[:].rearrange("p (n t) -> p n t", t=PACK)
-        q_bf = [reuse.tile([P, P * PACK], BF16, name="q_bf0", align_bytes=256, offset=0), keep.tile([P, P * PACK], BF16, name="q_bf1", align_bytes=64)]
-        u_codes = [keep.tile([P, CW], U32, name=f"u_codes{c}", align_bytes=256) for c in range(2)]
-        u_codes = u_codes + [reuse.tile([P, CW], U32, name=f"u_codes{c}", align_bytes=256, offset=4 * CW * (c - 2)) for c in range(2, NCH)]
+        q_bf = [keep.tile([P, P * PACK], BF16, name=f"q_bf{h}", align_bytes=64) for h in range(2)]
+        u_codes = [keep.tile([P, CW], U32, name=f"u_codes{c}", align_bytes=256) for c in range(NCH)]
         u_scales = [keep.tile([P, 64 + CW], U8, name=f"u_scales{c}", align_bytes=256)[:, 64:] for c in range(NCH)]
         q_codes = [keep.tile([P, P], U32, name=f"q_codes{h}", align_bytes=256) for h in range(2)]
         q_scales = [keep.tile([P, 192 + P], U8, name=f"q_scales{h}", align_bytes=256)[:, 192:] for h in range(2)]
@@ -73,6 +71,7 @@ def tile_attend_pre_edge_f_topk_kernel(tc, qT, kT, rT, ob, offs, offs2, out):
             return k_list[:, first // 16:last // 16]
 
         blocks = (0, 1, 2)
+        pieces = ((0, CW), (CW, POOL_AT - CW), (POOL_AT - CW, POOL_AT))
 
         def into_psum(name, parts, tag_turned, tag_back):
             turned = psum.tile([P, 3 * CW], F32, name=f"turned_{name}", tag=tag_turned)
@@ -88,7 +87,7 @@ def tile_attend_pre_edge_f_topk_kernel(tc, qT, kT, rT, ob, offs, offs2, out):
         for t in (3, 2, 1, 0):
             nc.vector.tensor_copy(r_g[:, t, :], r_tab[t // 2][:, t % 2, :].indirect(r_list[:]))
         r_top = into_psum("top", [r_g[:, 3, cols(c)] for c in blocks], "bank3", "bank4")
-        r_low = {c: into_psum(f"low{c}", [r_g[:, t, cols(c)] for t in range(3)], f"bank{b}", f"bank{5 + b}") for b, c in enumerate(blocks)}
+        r_low = [into_psum(f"low{b}", [r_g[:, t, first:first + CW] for t in range(3)], f"bank{b}", f"bank{5 + b}") for b, (first, last) in enumerate(pieces)]
 
         def gather_v(t, first, last):
             nc.vector.tensor_copy(k_g[:, t, first:last], k_tab[t][:].indirect(entries(first, last)))
@@ -96,11 +95,11 @@ def tile_attend_pre_edge_f_topk_kernel(tc, qT, kT, rT, ob, offs, offs2, out):
         def gather_s(t, first, last):
             nc.scalar.activation(k_g[:, t, first:last], k_tab[t][:].indirect(entries(first, last)), ACT.Copy)
 
-        def diff_low(first, last):
-            c = first // CW
+        def diff_low(b):
+            first, last = pieces[b]
             nc.vector.tensor_tensor(u_v[:, first:last, 0:3].rearrange("p (c i) t -> p c t i", i=2),
                                     k_g[:, 0:3, first:last].rearrange("p t (c i) -> p c t i", i=2),
-                                    r_low[c][:, :, first - c * CW:last - c * CW].rearrange("p t (c i) -> p c t i", i=2), ALU.subtract)
+                                    r_low[b][:, :, 0:last - first].rearrange("p t (c i) -> p c t i", i=2), ALU.subtract)
 
         def diff_g(t, first, last):
             nc.gpsimd.tensor_tensor(u_v[:, first:last, t], k_g[:, t, first:last], r_g[:, t, first:last], ALU.subtract)
@@ -115,9 +114,8 @@ def tile_attend_pre_edge_f_topk_kernel(tc, qT, kT, rT, ob, offs, offs2, out):
         gather_v(0, 0, CW)
         gather_v(0, CW, HALF)
         diff_g(0, POOL_AT, N)
-        diff_low(0, CW)
-        diff_low(HALF, POOL_AT)
-        diff_low(CW, HALF)
+        for b in range(3):
+            diff_low(b)
 
         for h in range(2):
             nc.scalar.copy(q_bf[h][:].rearrange("p (c i t) -> p c t i", i=4, t=PACK), q_raw[h][:].rearrange("p t (c i) -> p c t i", i=4))

@@ -28,6 +28,7 @@ def tile_attend_pre_edge_f_topk_kernel(tc, qT, kT, rT, ob, offs, offs2, out):
     with ExitStack() as ctx:
         lists = ctx.enter_context(tc.tile_pool(name="lists", bufs=1))
         keep = ctx.enter_context(tc.tile_pool(name="keep", bufs=1))
+        reuse = ctx.enter_context(tc.tile_pool(name="reuse", bufs=1))
         psum = ctx.enter_context(tc.psum_pool(name="psum", bufs=1))
 
         k_list = lists.tile([P, N // 16], U16, name="k_list")
@@ -37,7 +38,7 @@ def tile_attend_pre_edge_f_topk_kernel(tc, qT, kT, rT, ob, offs, offs2, out):
         q_rows = qT[0].rearrange("(p t) q -> p t q", t=PACK)
         r_tab = [keep.tile([P, 2, S], F32, name=f"r_tab{j}", align_bytes=256) for j in range(2)]
         k_tab = [keep.tile([P, T], F32, name=f"k_tab{t}", align_bytes=256) for t in range(PACK)]
-        q_raw = [keep.tile([P, PACK, P], F32, name=f"q_raw{h}", align_bytes=256) for h in range(2)]
+        q_raw = [reuse.tile([P, PACK, P], F32, name="q_raw0", align_bytes=256, offset=0), keep.tile([P, PACK, P], F32, name="q_raw1", align_bytes=256)]
         bias = [keep.tile([P, 1], F32, name=f"bias{h}") for h in range(2)]
 
         nc.sync.dma_start(r_tab[1][:], r_rows[:, 2:4, :])
@@ -58,7 +59,7 @@ def tile_attend_pre_edge_f_topk_kernel(tc, qT, kT, rT, ob, offs, offs2, out):
         u = keep.tile([P, N * PACK], BF16, name="u", align_bytes=64)
         u_v = u[:].rearrange("p (n t) -> p n t", t=PACK)
         q_bf = [keep.tile([P, P * PACK], BF16, name=f"q_bf{h}", align_bytes=64) for h in range(2)]
-        u_codes = [keep.tile([P, CW], U32, name=f"u_codes{c}", align_bytes=256) for c in range(NCH)]
+        u_codes = [reuse.tile([P, CW], U32, name=f"u_codes{c}", align_bytes=256, offset=4 * CW * c) for c in range(NCH)]
         u_scales = [keep.tile([P, 64 + CW], U8, name=f"u_scales{c}", align_bytes=256)[:, 64:] for c in range(NCH)]
         q_codes = [keep.tile([P, P], U32, name=f"q_codes{h}", align_bytes=256) for h in range(2)]
         q_scales = [keep.tile([P, 192 + P], U8, name=f"q_scales{h}", align_bytes=256)[:, 192:] for h in range(2)]
@@ -70,24 +71,23 @@ def tile_attend_pre_edge_f_topk_kernel(tc, qT, kT, rT, ob, offs, offs2, out):
         def entries(first, last):
             return k_list[:, first // 16:last // 16]
 
-        blocks = (0, 1, 2)
-        pieces = ((0, CW), (CW, POOL_AT - CW), (POOL_AT - CW, POOL_AT))
-
         def into_psum(name, parts, tag_turned, tag_back):
-            turned = psum.tile([P, 3 * CW], F32, name=f"turned_{name}", tag=tag_turned)
-            held = keep.tile([P, 3 * CW], F32, name=f"held_{name}")
-            back = psum.tile([P, 3 * CW], F32, name=f"back_{name}", tag=tag_back)
+            width = len(parts) * CW
+            turned = psum.tile([P, width], F32, name=f"turned_{name}", tag=tag_turned)
+            held = keep.tile([P, width], F32, name=f"held_{name}")
+            back = psum.tile([P, width], F32, name=f"back_{name}", tag=tag_back)
             for b, part in enumerate(parts):
                 nc.tensor.transpose(turned[:, cols(b)], part, ident[:])
             nc.scalar.copy(held[:], turned[:])
-            for b in range(3):
+            for b in range(len(parts)):
                 nc.tensor.transpose(back[:, cols(b)], held[:, cols(b)], ident[:])
-            return back[:].rearrange("p (b n) -> p b n", b=3)
+            return back
 
         for t in (3, 2, 1, 0):
             nc.vector.tensor_copy(r_g[:, t, :], r_tab[t // 2][:, t % 2, :].indirect(r_list[:]))
-        r_top = into_psum("top", [r_g[:, 3, cols(c)] for c in blocks], "bank3", "bank4")
-        r_low = [into_psum(f"low{b}", [r_g[:, t, first:first + CW] for t in range(3)], f"bank{b}", f"bank{5 + b}") for b, (first, last) in enumerate(pieces)]
+        r_top = [into_psum("front", [r_g[:, t, cols(c)] for t in (2, 3) for c in range(2)], "bank2", "bank4"),
+                 into_psum("rest", [r_g[:, t, cols(2)] for t in (2, 3)], "bank3", "bank5")]
+        r_ps = {t: into_psum(f"r{t}", [r_g[:, t, cols(c)] for c in range(3)], f"bank{t}", f"bank{7 - t}") for t in (1, 0)}
 
         def gather_v(t, first, last):
             nc.vector.tensor_copy(k_g[:, t, first:last], k_tab[t][:].indirect(entries(first, last)))
@@ -95,27 +95,29 @@ def tile_attend_pre_edge_f_topk_kernel(tc, qT, kT, rT, ob, offs, offs2, out):
         def gather_s(t, first, last):
             nc.scalar.activation(k_g[:, t, first:last], k_tab[t][:].indirect(entries(first, last)), ACT.Copy)
 
-        def diff_low(b):
-            first, last = pieces[b]
-            nc.vector.tensor_tensor(u_v[:, first:last, 0:3].rearrange("p (c i) t -> p c t i", i=2),
-                                    k_g[:, 0:3, first:last].rearrange("p t (c i) -> p c t i", i=2),
-                                    r_low[b][:, :, 0:last - first].rearrange("p t (c i) -> p c t i", i=2), ALU.subtract)
+        def diff_v(t, first, last):
+            nc.vector.tensor_tensor(u_v[:, first:last, t], k_g[:, t, first:last], r_ps[t][:, first:last], ALU.subtract)
 
         def diff_g(t, first, last):
             nc.gpsimd.tensor_tensor(u_v[:, first:last, t], k_g[:, t, first:last], r_g[:, t, first:last], ALU.subtract)
 
         for t in (3, 2, 1):
-            gather_v(t, 0, HALF)
-            gather_s(t, HALF, N)
+            gather_v(t, 0, POOL_AT)
+            gather_s(t, POOL_AT, N)
             diff_g(t, POOL_AT, N)
-        nc.vector.tensor_tensor(u_v[:, 0:POOL_AT, 3], k_g[:, 3, 0:POOL_AT], r_top.rearrange("p b n -> p (b n)")[:, 0:POOL_AT], ALU.subtract)
+            if t == 2:
+                for top, first, last in ((r_top[0], 0, HALF), (r_top[1], HALF, POOL_AT)):
+                    nc.vector.tensor_tensor(u_v[:, first:last, 2:4].rearrange("p (c i) t -> p c t i", i=2),
+                                            k_g[:, 2:4, first:last].rearrange("p t (c i) -> p c t i", i=2),
+                                            top[:].rearrange("p (t n) -> p t n", t=2)[:, :, 0:last - first].rearrange("p t (c i) -> p c t i", i=2), ALU.subtract)
+        diff_v(1, 0, POOL_AT)
         gather_s(0, POOL_AT, N)
         gather_s(0, HALF, POOL_AT)
         gather_v(0, 0, CW)
         gather_v(0, CW, HALF)
         diff_g(0, POOL_AT, N)
-        for b in range(3):
-            diff_low(b)
+        diff_v(0, 0, CW)
+        diff_v(0, CW, POOL_AT)
 
         for h in range(2):
             nc.scalar.copy(q_bf[h][:].rearrange("p (c i t) -> p c t i", i=4, t=PACK), q_raw[h][:].rearrange("p t (c i) -> p c t i", i=4))

@@ -20,7 +20,9 @@ PACK = 4
 HALF = N // 2
 CW = 128
 NCH = N // CW
-POOL_AT = HALF + 64
+POOL_END = CW + 32
+LATE = 3 * CW
+PAD = 64
 
 
 def tile_attend_pre_edge_f_topk_kernel(tc, qT, kT, rT, ob, offs, offs2, out):
@@ -33,20 +35,20 @@ def tile_attend_pre_edge_f_topk_kernel(tc, qT, kT, rT, ob, offs, offs2, out):
 
         k_list = lists.tile([P, N // 16], U16, name="k_list")
         r_list = lists.tile([P, N // 16], U16, name="r_list")
-        r_rows = rT.rearrange("(p t) s -> p t s", t=PACK)
         k_rows = kT.rearrange("(p t) s -> p t s", t=PACK)
         q_rows = qT[0].rearrange("(p t) q -> p t q", t=PACK)
-        r_tab = [keep.tile([P, 2, S], F32, name=f"r_tab{j}", align_bytes=256) for j in range(2)]
-        k_tab = [keep.tile([P, T], F32, name=f"k_tab{t}", align_bytes=256) for t in range(PACK)]
-        q_raw = [reuse.tile([P, PACK, P], F32, name="q_raw0", align_bytes=256, offset=0), keep.tile([P, PACK, P], F32, name="q_raw1", align_bytes=256)]
+        r_tab = keep.tile([P, 2, 2 * S + PAD], F32, name="r_tab", align_bytes=256)
+        k_top = keep.tile([P, 2, T + PAD], F32, name="k_top", align_bytes=256)
+        k_low = [keep.tile([P, T], F32, name=f"k_low{t}", align_bytes=256) for t in range(2)]
+        q_raw = [reuse.tile([P, PACK, P], F32, name="q_raw0", align_bytes=256, offset=0), reuse.tile([P, PACK, P], F32, name="q_raw1", align_bytes=256, offset=4 * PACK * P)]
         bias = [keep.tile([P, 1], F32, name=f"bias{h}") for h in range(2)]
 
-        nc.sync.dma_start(r_tab[1][:], r_rows[:, 2:4, :])
+        nc.sync.dma_start(r_tab[:, :, 0:2 * S], rT.rearrange("(p j t) s -> p j (t s)", j=2, t=2))
         nc.sync.dma_start(r_list[:], offs2)
-        nc.sync.dma_start(r_tab[0][:], r_rows[:, 0:2, :])
         nc.sync.dma_start(k_list[:], offs)
-        for t in (3, 2, 1, 0):
-            nc.sync.dma_start(k_tab[t][:], k_rows[:, t, :])
+        nc.sync.dma_start(k_top[:, :, 0:T], k_rows[:, 2:4, :])
+        for t in (1, 0):
+            nc.sync.dma_start(k_low[t][:], k_rows[:, t, :])
         for h in range(2):
             nc.sync.dma_start(q_raw[h][:], q_rows[:, :, h * P:(h + 1) * P])
         for h in range(2):
@@ -56,94 +58,128 @@ def tile_attend_pre_edge_f_topk_kernel(tc, qT, kT, rT, ob, offs, offs2, out):
         make_identity(nc, ident[:])
         r_g = keep.tile([P, PACK, N], F32, name="r_g")
         k_g = keep.tile([P, PACK, N], F32, name="k_g")
-        u = keep.tile([P, N * PACK], BF16, name="u", align_bytes=64)
+        u = keep.tile([P, LATE * PACK], BF16, name="u", align_bytes=64)
+        u_late = reuse.tile([P, CW * PACK], BF16, name="u_late", align_bytes=256, offset=4 * PACK * P + 4 * 2 * CW)
+        pairs = reuse.tile([P, 2, CW * 2], BF16, name="pairs", align_bytes=256, offset=8 * PACK * P + 4 * CW)
         u_v = u[:].rearrange("p (n t) -> p n t", t=PACK)
         q_bf = [keep.tile([P, P * PACK], BF16, name=f"q_bf{h}", align_bytes=64) for h in range(2)]
-        u_codes = [reuse.tile([P, CW], U32, name=f"u_codes{c}", align_bytes=256, offset=4 * CW * c) for c in range(NCH)]
+        u_codes = [keep.tile([P, CW], U32, name="u_codes0", align_bytes=256)]
+        u_codes = u_codes + [reuse.tile([P, CW], U32, name=f"u_codes{c}", align_bytes=256, offset=4 * PACK * P * (c - 1)) for c in (1, 2)]
+        u_codes = u_codes + [keep.tile([P, CW], U32, name="u_codes3", align_bytes=256)]
         u_scales = [keep.tile([P, 64 + CW], U8, name=f"u_scales{c}", align_bytes=256)[:, 64:] for c in range(NCH)]
         q_codes = [keep.tile([P, P], U32, name=f"q_codes{h}", align_bytes=256) for h in range(2)]
         q_scales = [keep.tile([P, 192 + P], U8, name=f"q_scales{h}", align_bytes=256)[:, 192:] for h in range(2)]
-        res = [[keep.tile([P, HALF], F32, name=f"res{h}_{j}", align_bytes=256) for j in range(2)] for h in range(2)]
+        res = [reuse.tile([P, 2, CW], F32, name=f"res{j}", align_bytes=256, offset=8 * PACK * P + 8 * CW * j) for j in range(2)]
+        res = res + [reuse.tile([P, 2, CW], F32, name="res2", align_bytes=256, offset=4 * PACK * P + 4 * 2 * CW)]
+        res = res + [keep.tile([P, 2, CW], F32, name="res3", align_bytes=256)]
 
         def cols(c):
             return slice(c * CW, (c + 1) * CW)
 
-        def entries(first, last):
-            return k_list[:, first // 16:last // 16]
+        def r_plane(t):
+            return r_tab[:, t // 2, (t % 2) * S:(t % 2 + 1) * S]
 
-        def into_psum(name, parts, tag_turned, tag_back):
-            width = len(parts) * CW
-            turned = psum.tile([P, width], F32, name=f"turned_{name}", tag=tag_turned)
-            held = keep.tile([P, width], F32, name=f"held_{name}")
-            back = psum.tile([P, width], F32, name=f"back_{name}", tag=tag_back)
-            for b, part in enumerate(parts):
-                nc.tensor.transpose(turned[:, cols(b)], part, ident[:])
-            nc.scalar.copy(held[:], turned[:])
-            for b in range(len(parts)):
+        def k_plane(t):
+            return k_top[:, t - 2, 0:T] if t >= 2 else k_low[t][:]
+
+        def gather_v(t, first, last):
+            nc.vector.tensor_copy(k_g[:, t, first:last], k_plane(t).indirect(k_list[:, first // 16:last // 16]))
+
+        def gather_s(t, first, last):
+            nc.scalar.activation(k_g[:, t, first:last], k_plane(t).indirect(k_list[:, first // 16:last // 16]), ACT.Copy)
+
+        def into_psum(t):
+            turned = psum.tile([P, 3 * CW], F32, name=f"turned{t}", tag=f"bank{t}")
+            held = keep.tile([P, 3 * CW], F32, name=f"held{t}")
+            back = psum.tile([P, 3 * CW], F32, name=f"back{t}", tag=f"bank{7 - t}")
+            for b in range(3):
+                nc.tensor.transpose(turned[:, cols(b)], r_g[:, t, cols(b + 1)], ident[:])
+            nc.vector.tensor_copy(held[:], turned[:])
+            for b in range(3):
                 nc.tensor.transpose(back[:, cols(b)], held[:, cols(b)], ident[:])
             return back
 
-        for t in (3, 2, 1, 0):
-            nc.vector.tensor_copy(r_g[:, t, :], r_tab[t // 2][:, t % 2, :].indirect(r_list[:]))
-        r_top = [into_psum("front", [r_g[:, t, cols(c)] for t in (2, 3) for c in range(2)], "bank2", "bank4"),
-                 into_psum("rest", [r_g[:, t, cols(2)] for t in (2, 3)], "bank3", "bank5")]
-        r_ps = {t: into_psum(f"r{t}", [r_g[:, t, cols(c)] for c in range(3)], f"bank{t}", f"bank{7 - t}") for t in (1, 0)}
-
-        def gather_v(t, first, last):
-            nc.vector.tensor_copy(k_g[:, t, first:last], k_tab[t][:].indirect(entries(first, last)))
-
-        def gather_s(t, first, last):
-            nc.scalar.activation(k_g[:, t, first:last], k_tab[t][:].indirect(entries(first, last)), ACT.Copy)
+        for t in (1, 0):
+            nc.vector.tensor_copy(r_g[:, t, :], r_plane(t).indirect(r_list[:]))
+        for t in (3, 2):
+            nc.scalar.activation(r_g[:, t, :], r_plane(t).indirect(r_list[:]), ACT.Copy)
+        r_ps = {t: into_psum(t) for t in (1, 0)}
 
         def diff_v(t, first, last):
-            nc.vector.tensor_tensor(u_v[:, first:last, t], k_g[:, t, first:last], r_ps[t][:, first:last], ALU.subtract)
+            nc.vector.tensor_tensor(u_v[:, first:last, t], k_g[:, t, first:last], r_ps[t][:, first - CW:last - CW], ALU.subtract)
 
         def diff_g(t, first, last):
             nc.gpsimd.tensor_tensor(u_v[:, first:last, t], k_g[:, t, first:last], r_g[:, t, first:last], ALU.subtract)
 
-        for t in (3, 2, 1):
-            gather_v(t, 0, POOL_AT)
-            gather_s(t, POOL_AT, N)
-            diff_g(t, POOL_AT, N)
-            if t == 2:
-                for top, first, last in ((r_top[0], 0, HALF), (r_top[1], HALF, POOL_AT)):
-                    nc.vector.tensor_tensor(u_v[:, first:last, 2:4].rearrange("p (c i) t -> p c t i", i=2),
-                                            k_g[:, 2:4, first:last].rearrange("p t (c i) -> p c t i", i=2),
-                                            top[:].rearrange("p (t n) -> p t n", t=2)[:, :, 0:last - first].rearrange("p t (c i) -> p c t i", i=2), ALU.subtract)
-        diff_v(1, 0, POOL_AT)
-        gather_s(0, POOL_AT, N)
-        gather_s(0, HALF, POOL_AT)
-        gather_v(0, 0, CW)
-        gather_v(0, CW, HALF)
-        diff_g(0, POOL_AT, N)
-        diff_v(0, 0, CW)
-        diff_v(0, CW, POOL_AT)
+        def diff_late(t):
+            nc.vector.tensor_tensor(pairs[:, 0, :].rearrange("p (n t) -> p n t", t=2)[:, :, t], k_g[:, t, LATE:N], r_ps[t][:, LATE - CW:N - CW], ALU.subtract)
+
+        def diff_top(engine, first, last):
+            engine.tensor_tensor(u_v[:, first:last, 2:4].rearrange("p (c i) t -> p c t i", i=2),
+                                 k_g[:, 2:4, first:last].rearrange("p t (c i) -> p c t i", i=2),
+                                 r_g[:, 2:4, first:last].rearrange("p t (c i) -> p c t i", i=2), ALU.subtract)
+
+        gather_v(3, POOL_END, N)
+        gather_s(2, POOL_END, N)
+        diff_top(nc.vector, POOL_END, LATE)
+        nc.vector.tensor_tensor(pairs[:, 1, :].rearrange("p (c i t) -> p c t i", i=2, t=2), k_g[:, 2:4, LATE:N].rearrange("p t (c i) -> p c t i", i=2),
+                                r_g[:, 2:4, LATE:N].rearrange("p t (c i) -> p c t i", i=2), ALU.subtract)
+        for t in (3, 2):
+            gather_s(t, 0, POOL_END)
+        diff_top(nc.gpsimd, 0, POOL_END)
+
+        gather_s(1, 0, POOL_END)
+        gather_v(1, HALF, LATE)
+        gather_s(1, LATE, N)
+        gather_s(1, POOL_END, HALF)
+        diff_g(1, 0, POOL_END)
+        diff_v(1, HALF, LATE)
+        diff_late(1)
+        diff_v(1, POOL_END, HALF)
+
+        gather_s(0, 0, POOL_END)
+        gather_v(0, HALF, LATE)
+        gather_v(0, LATE, N)
+        gather_s(0, POOL_END, HALF)
+        diff_g(0, 0, POOL_END)
+        diff_v(0, HALF, LATE)
+        diff_v(0, POOL_END, HALF)
+        diff_late(0)
 
         for h in range(2):
             nc.scalar.copy(q_bf[h][:].rearrange("p (c i t) -> p c t i", i=4, t=PACK), q_raw[h][:].rearrange("p t (c i) -> p c t i", i=4))
+        nc.scalar.copy(u_late[:].bitcast(U32).rearrange("p (c i w) -> p c w i", i=2, w=2),
+                       pairs[:].rearrange("p w n -> p (w n)").bitcast(U32).rearrange("p (w c i) -> p c w i", w=2, i=2))
 
         def quant_u(c):
-            woven = u[:, c * CW * PACK:(c + 1) * CW * PACK]
+            woven = u[:, c * CW * PACK:(c + 1) * CW * PACK] if c * CW < LATE else u_late[:]
             nc.vector.quantize_mx(out=u_codes[c][:].bitcast(FP8X4), scales=u_scales[c], in_=woven)
 
         def quant_q(h):
             nc.vector.quantize_mx(out=q_codes[h][:].bitcast(FP8X4), scales=q_scales[h], in_=q_bf[h][:])
 
-        quant_u(0)
-        quant_q(0)
-        for c in range(1, NCH):
+        for c in range(2):
             quant_u(c)
-        quant_q(1)
+            quant_q(c)
+        quant_u(2)
+        quant_u(3)
 
-        for h in range(2):
-            for c in range(NCH):
-                acc = psum.tile([P, CW], F32, name=f"acc{h}_{c}", tag=f"bank{NCH * h + c}")
-                nc.tensor.matmul_mx(out=acc[:], lhsT=q_codes[h][:].bitcast(FP8X4), lhsT_scale=q_scales[h],
-                                    rhs=u_codes[c][:].bitcast(FP8X4), rhs_scale=u_scales[c], start=True, stop=True)
-                dst = res[h][c // 2][:, cols(c % 2)]
-                if h == 1 and c % 2 == 0:
-                    nc.vector.tensor_scalar(dst, acc[:], bias[h][:], 0.0, ALU.add, ALU.max)
-                else:
-                    nc.scalar.activation(dst, acc[:], ACT.Relu, bias=bias[h][:])
-                if c % 2 == 1:
-                    nc.sync.dma_start(out[0, h * P:(h + 1) * P, (c // 2) * HALF:(c // 2 + 1) * HALF], res[h][c // 2][:])
+        def product(h, c, dst, bank):
+            acc = psum.tile([P, CW], F32, name=f"acc{h}_{c}", tag=f"bank{bank}")
+            nc.tensor.matmul_mx(out=acc[:], lhsT=q_codes[h][:].bitcast(FP8X4), lhsT_scale=q_scales[h],
+                                rhs=u_codes[c][:].bitcast(FP8X4), rhs_scale=u_scales[c], start=True, stop=True)
+            if h == 0 and c >= 2:
+                nc.vector.tensor_scalar(dst, acc[:], bias[h][:], 0.0, ALU.add, ALU.max)
+            else:
+                nc.scalar.activation(dst, acc[:], ACT.Relu, bias=bias[h][:])
+
+        for c in range(2):
+            product(0, c, res[0][:, c, :], c)
+            nc.sync.dma_start(out[0, 0:P, cols(c)], res[0][:, c, :])
+        for c in range(2):
+            product(1, c, res[1][:, c, :], 2 + c)
+        nc.sync.dma_start(out[0, P:2 * P, 0:HALF], res[1][:].rearrange("p c n -> p (c n)"))
+        for c in (2, 3):
+            for h in range(2):
+                product(h, c, res[c][:, h, :], 2 * c + h)
+            nc.sync.dma_start(out[0, :, cols(c)].rearrange("(h p) n -> p h n", h=2), res[c][:])

@@ -121,9 +121,9 @@ def tile_attend_pre_edge_f_topk_kernel(tc, qT, kT, rT, ob, offs, offs2, out):
 
         gather_v(3, POOL_END, N)
         gather_s(2, POOL_END, N)
-        diff_top(nc.vector, POOL_END, LATE)
         nc.vector.tensor_tensor(pairs[:, 1, :].rearrange("p (c i t) -> p c t i", i=2, t=2), k_g[:, 2:4, LATE:N].rearrange("p t (c i) -> p c t i", i=2),
                                 r_g[:, 2:4, LATE:N].rearrange("p t (c i) -> p c t i", i=2), ALU.subtract)
+        diff_top(nc.vector, POOL_END, LATE)
         for t in (3, 2):
             gather_s(t, 0, POOL_END)
         diff_top(nc.gpsimd, 0, POOL_END)

@@ -22,7 +22,6 @@ CW = 128
 NCH = N // CW
 POOL_END = CW + 32
 LATE = 3 * CW
-PAD = 64
 
 
 def tile_attend_pre_edge_f_topk_kernel(tc, qT, kT, rT, ob, offs, offs2, out):
@@ -37,18 +36,18 @@ def tile_attend_pre_edge_f_topk_kernel(tc, qT, kT, rT, ob, offs, offs2, out):
         r_list = lists.tile([P, N // 16], U16, name="r_list")
         k_rows = kT.rearrange("(p t) s -> p t s", t=PACK)
         q_rows = qT[0].rearrange("(p t) q -> p t q", t=PACK)
-        r_tab = keep.tile([P, 2, 2 * S + PAD], F32, name="r_tab", align_bytes=256)
-        k_top = keep.tile([P, 2, T + PAD], F32, name="k_top", align_bytes=256)
-        k_low = [keep.tile([P, T], F32, name=f"k_low{t}", align_bytes=256) for t in range(2)]
+        r_rows = rT.rearrange("(p t) s -> p t s", t=PACK)
+        r_tab = [keep.tile([P, 2, S], F32, name=f"r_tab{j}", align_bytes=256) for j in range(2)]
+        k_tab = [keep.tile([P, T], F32, name=f"k_tab{t}", align_bytes=256) for t in range(PACK)]
         q_raw = [reuse.tile([P, PACK, P], F32, name="q_raw0", align_bytes=256, offset=0), reuse.tile([P, PACK, P], F32, name="q_raw1", align_bytes=256, offset=4 * PACK * P)]
         bias = [keep.tile([P, 1], F32, name=f"bias{h}") for h in range(2)]
 
-        nc.sync.dma_start(r_tab[:, :, 0:2 * S], rT.rearrange("(p j t) s -> p j (t s)", j=2, t=2))
+        nc.sync.dma_start(r_tab[1][:], r_rows[:, 2:4, :])
         nc.sync.dma_start(r_list[:], offs2)
+        nc.sync.dma_start(r_tab[0][:], r_rows[:, 0:2, :])
         nc.sync.dma_start(k_list[:], offs)
-        nc.sync.dma_start(k_top[:, :, 0:T], k_rows[:, 2:4, :])
-        for t in (1, 0):
-            nc.sync.dma_start(k_low[t][:], k_rows[:, t, :])
+        for t in (3, 2, 1, 0):
+            nc.sync.dma_start(k_tab[t][:], k_rows[:, t, :])
         for h in range(2):
             nc.sync.dma_start(q_raw[h][:], q_rows[:, :, h * P:(h + 1) * P])
         for h in range(2):
@@ -76,17 +75,11 @@ def tile_attend_pre_edge_f_topk_kernel(tc, qT, kT, rT, ob, offs, offs2, out):
         def cols(c):
             return slice(c * CW, (c + 1) * CW)
 
-        def r_plane(t):
-            return r_tab[:, t // 2, (t % 2) * S:(t % 2 + 1) * S]
-
-        def k_plane(t):
-            return k_top[:, t - 2, 0:T] if t >= 2 else k_low[t][:]
-
         def gather_v(t, first, last):
-            nc.vector.tensor_copy(k_g[:, t, first:last], k_plane(t).indirect(k_list[:, first // 16:last // 16]))
+            nc.vector.tensor_copy(k_g[:, t, first:last], k_tab[t][:].indirect(k_list[:, first // 16:last // 16]))
 
         def gather_s(t, first, last):
-            nc.scalar.activation(k_g[:, t, first:last], k_plane(t).indirect(k_list[:, first // 16:last // 16]), ACT.Copy)
+            nc.scalar.activation(k_g[:, t, first:last], k_tab[t][:].indirect(k_list[:, first // 16:last // 16]), ACT.Copy)
 
         def into_psum(t):
             turned = psum.tile([P, 3 * CW], F32, name=f"turned{t}", tag=f"bank{t}")
@@ -94,15 +87,13 @@ def tile_attend_pre_edge_f_topk_kernel(tc, qT, kT, rT, ob, offs, offs2, out):
             back = psum.tile([P, 3 * CW], F32, name=f"back{t}", tag=f"bank{7 - t}")
             for b in range(3):
                 nc.tensor.transpose(turned[:, cols(b)], r_g[:, t, cols(b + 1)], ident[:])
-            nc.vector.tensor_copy(held[:], turned[:])
+            nc.scalar.copy(held[:], turned[:])
             for b in range(3):
                 nc.tensor.transpose(back[:, cols(b)], held[:, cols(b)], ident[:])
             return back
 
-        for t in (1, 0):
-            nc.vector.tensor_copy(r_g[:, t, :], r_plane(t).indirect(r_list[:]))
-        for t in (3, 2):
-            nc.scalar.activation(r_g[:, t, :], r_plane(t).indirect(r_list[:]), ACT.Copy)
+        for t in (3, 2, 1, 0):
+            nc.vector.tensor_copy(r_g[:, t, :], r_tab[t // 2][:, t % 2, :].indirect(r_list[:]))
         r_ps = {t: into_psum(t) for t in (1, 0)}
 
         def diff_v(t, first, last):
@@ -114,19 +105,18 @@ def tile_attend_pre_edge_f_topk_kernel(tc, qT, kT, rT, ob, offs, offs2, out):
         def diff_late(t):
             nc.vector.tensor_tensor(pairs[:, 0, :].rearrange("p (n t) -> p n t", t=2)[:, :, t], k_g[:, t, LATE:N], r_ps[t][:, LATE - CW:N - CW], ALU.subtract)
 
-        def diff_top(engine, first, last):
-            engine.tensor_tensor(u_v[:, first:last, 2:4].rearrange("p (c i) t -> p c t i", i=2),
-                                 k_g[:, 2:4, first:last].rearrange("p t (c i) -> p c t i", i=2),
-                                 r_g[:, 2:4, first:last].rearrange("p t (c i) -> p c t i", i=2), ALU.subtract)
+        def diff_top(woven, first, last):
+            nc.vector.tensor_tensor(woven.rearrange("p (c i) t -> p c t i", i=2), k_g[:, 2:4, first:last].rearrange("p t (c i) -> p c t i", i=2),
+                                    r_g[:, 2:4, first:last].rearrange("p t (c i) -> p c t i", i=2), ALU.subtract)
 
-        gather_v(3, POOL_END, N)
-        gather_s(2, POOL_END, N)
-        nc.vector.tensor_tensor(pairs[:, 1, :].rearrange("p (c i t) -> p c t i", i=2, t=2), k_g[:, 2:4, LATE:N].rearrange("p t (c i) -> p c t i", i=2),
-                                r_g[:, 2:4, LATE:N].rearrange("p t (c i) -> p c t i", i=2), ALU.subtract)
-        diff_top(nc.vector, POOL_END, LATE)
         for t in (3, 2):
+            gather_v(t, POOL_END, LATE)
+            gather_s(t, LATE, N)
             gather_s(t, 0, POOL_END)
-        diff_top(nc.gpsimd, 0, POOL_END)
+            if t == 2:
+                diff_top(pairs[:, 1, :].rearrange("p (n t) -> p n t", t=2), LATE, N)
+                diff_top(u_v[:, POOL_END:LATE, 2:4], POOL_END, LATE)
+            diff_g(t, 0, POOL_END)
 
         gather_s(1, 0, POOL_END)
         gather_v(1, HALF, LATE)
@@ -173,12 +163,10 @@ def tile_attend_pre_edge_f_topk_kernel(tc, qT, kT, rT, ob, offs, offs2, out):
             else:
                 nc.scalar.activation(dst, acc[:], ACT.Relu, bias=bias[h][:])
 
-        for c in range(2):
-            product(0, c, res[0][:, c, :], c)
-            nc.sync.dma_start(out[0, 0:P, cols(c)], res[0][:, c, :])
-        for c in range(2):
-            product(1, c, res[1][:, c, :], 2 + c)
-        nc.sync.dma_start(out[0, P:2 * P, 0:HALF], res[1][:].rearrange("p c n -> p (c n)"))
+        for h in range(2):
+            for c in range(2):
+                product(h, c, res[h][:, c, :], 2 * h + c)
+            nc.sync.dma_start(out[0, h * P:(h + 1) * P, 0:HALF], res[h][:].rearrange("p c n -> p (c n)"))
         for c in (2, 3):
             for h in range(2):
                 product(h, c, res[c][:, h, :], 2 * c + h)

@@ -39,7 +39,7 @@ def tile_attend_pre_edge_f_topk_kernel(tc, qT, kT, rT, ob, offs, offs2, out):
         r_rows = rT.rearrange("(p t) s -> p t s", t=PACK)
         r_tab = [keep.tile([P, 2, S], F32, name=f"r_tab{j}", align_bytes=256) for j in range(2)]
         k_tab = [keep.tile([P, T], F32, name=f"k_tab{t}", align_bytes=256) for t in range(PACK)]
-        q_raw = [reuse.tile([P, PACK, P], F32, name="q_raw0", align_bytes=256, offset=0), reuse.tile([P, PACK, P], F32, name="q_raw1", align_bytes=256, offset=4 * PACK * P)]
+        q_raw = [reuse.tile([P, PACK, P], F32, name="q_raw0", align_bytes=256, offset=0), keep.tile([P, PACK, P], F32, name="q_raw1", align_bytes=256)]
         bias = [keep.tile([P, 1], F32, name=f"bias{h}") for h in range(2)]
 
         nc.sync.dma_start(r_tab[1][:], r_rows[:, 2:4, :])
@@ -58,19 +58,16 @@ def tile_attend_pre_edge_f_topk_kernel(tc, qT, kT, rT, ob, offs, offs2, out):
         r_g = keep.tile([P, PACK, N], F32, name="r_g")
         k_g = keep.tile([P, PACK, N], F32, name="k_g")
         u = keep.tile([P, LATE * PACK], BF16, name="u", align_bytes=64)
-        u_late = reuse.tile([P, CW * PACK], BF16, name="u_late", align_bytes=256, offset=4 * PACK * P + 4 * 2 * CW)
-        pairs = reuse.tile([P, 2, CW * 2], BF16, name="pairs", align_bytes=256, offset=8 * PACK * P + 4 * CW)
+        u_late = keep.tile([P, CW * PACK], BF16, name="u_late", align_bytes=64)
+        pairs = keep.tile([P, 2, CW * 2], BF16, name="pairs", align_bytes=64)
         u_v = u[:].rearrange("p (n t) -> p n t", t=PACK)
         q_bf = [keep.tile([P, P * PACK], BF16, name=f"q_bf{h}", align_bytes=64) for h in range(2)]
         u_codes = [keep.tile([P, CW], U32, name="u_codes0", align_bytes=256)]
-        u_codes = u_codes + [reuse.tile([P, CW], U32, name=f"u_codes{c}", align_bytes=256, offset=4 * PACK * P * (c - 1)) for c in (1, 2)]
-        u_codes = u_codes + [keep.tile([P, CW], U32, name="u_codes3", align_bytes=256)]
+        u_codes = u_codes + [reuse.tile([P, CW], U32, name=f"u_codes{c}", align_bytes=256, offset=4 * CW * c) for c in range(1, NCH)]
         u_scales = [keep.tile([P, 64 + CW], U8, name=f"u_scales{c}", align_bytes=256)[:, 64:] for c in range(NCH)]
         q_codes = [keep.tile([P, P], U32, name=f"q_codes{h}", align_bytes=256) for h in range(2)]
         q_scales = [keep.tile([P, 192 + P], U8, name=f"q_scales{h}", align_bytes=256)[:, 192:] for h in range(2)]
-        res = [reuse.tile([P, 2, CW], F32, name=f"res{j}", align_bytes=256, offset=8 * PACK * P + 8 * CW * j) for j in range(2)]
-        res = res + [reuse.tile([P, 2, CW], F32, name="res2", align_bytes=256, offset=4 * PACK * P + 4 * 2 * CW)]
-        res = res + [keep.tile([P, 2, CW], F32, name="res3", align_bytes=256)]
+        res = [[keep.tile([P, HALF], F32, name=f"res{h}_{j}", align_bytes=256) for j in range(2)] for h in range(2)]
 
         def cols(c):
             return slice(c * CW, (c + 1) * CW)
@@ -128,18 +125,21 @@ def tile_attend_pre_edge_f_topk_kernel(tc, qT, kT, rT, ob, offs, offs2, out):
         diff_v(1, POOL_END, HALF)
 
         gather_s(0, 0, POOL_END)
-        gather_v(0, HALF, LATE)
         gather_v(0, LATE, N)
+        gather_v(0, HALF, LATE)
         gather_s(0, POOL_END, HALF)
         diff_g(0, 0, POOL_END)
+        diff_late(0)
         diff_v(0, HALF, LATE)
         diff_v(0, POOL_END, HALF)
-        diff_late(0)
 
-        for h in range(2):
+        def cast_q(h):
             nc.scalar.copy(q_bf[h][:].rearrange("p (c i t) -> p c t i", i=4, t=PACK), q_raw[h][:].rearrange("p t (c i) -> p c t i", i=4))
+
+        cast_q(0)
         nc.scalar.copy(u_late[:].bitcast(U32).rearrange("p (c i w) -> p c w i", i=2, w=2),
                        pairs[:].rearrange("p w n -> p (w n)").bitcast(U32).rearrange("p (w c i) -> p c w i", w=2, i=2))
+        cast_q(1)
 
         def quant_u(c):
             woven = u[:, c * CW * PACK:(c + 1) * CW * PACK] if c * CW < LATE else u_late[:]
@@ -148,26 +148,21 @@ def tile_attend_pre_edge_f_topk_kernel(tc, qT, kT, rT, ob, offs, offs2, out):
         def quant_q(h):
             nc.vector.quantize_mx(out=q_codes[h][:].bitcast(FP8X4), scales=q_scales[h], in_=q_bf[h][:])
 
-        for c in range(2):
+        quant_u(0)
+        quant_q(0)
+        for c in range(1, NCH):
             quant_u(c)
-            quant_q(c)
-        quant_u(2)
-        quant_u(3)
-
-        def product(h, c, dst, bank):
-            acc = psum.tile([P, CW], F32, name=f"acc{h}_{c}", tag=f"bank{bank}")
-            nc.tensor.matmul_mx(out=acc[:], lhsT=q_codes[h][:].bitcast(FP8X4), lhsT_scale=q_scales[h],
-                                rhs=u_codes[c][:].bitcast(FP8X4), rhs_scale=u_scales[c], start=True, stop=True)
-            if h == 0 and c >= 2:
-                nc.vector.tensor_scalar(dst, acc[:], bias[h][:], 0.0, ALU.add, ALU.max)
-            else:
-                nc.scalar.activation(dst, acc[:], ACT.Relu, bias=bias[h][:])
+        quant_q(1)
 
         for h in range(2):
-            for c in range(2):
-                product(h, c, res[h][:, c, :], 2 * h + c)
-            nc.sync.dma_start(out[0, h * P:(h + 1) * P, 0:HALF], res[h][:].rearrange("p c n -> p (c n)"))
-        for c in (2, 3):
-            for h in range(2):
-                product(h, c, res[c][:, h, :], 2 * c + h)
-            nc.sync.dma_start(out[0, :, cols(c)].rearrange("(h p) n -> p h n", h=2), res[c][:])
+            for c in range(NCH):
+                acc = psum.tile([P, CW], F32, name=f"acc{h}_{c}", tag=f"bank{NCH * h + c}")
+                nc.tensor.matmul_mx(out=acc[:], lhsT=q_codes[h][:].bitcast(FP8X4), lhsT_scale=q_scales[h],
+                                    rhs=u_codes[c][:].bitcast(FP8X4), rhs_scale=u_scales[c], start=True, stop=True)
+                dst = res[h][c // 2][:, cols(c % 2)]
+                if h == 1 and c % 2 == 0:
+                    nc.vector.tensor_scalar(dst, acc[:], bias[h][:], 0.0, ALU.add, ALU.max)
+                else:
+                    nc.scalar.activation(dst, acc[:], ACT.Relu, bias=bias[h][:])
+                if c % 2 == 1:
+                    nc.sync.dma_start(out[0, h * P:(h + 1) * P, (c // 2) * HALF:(c // 2 + 1) * HALF], res[h][c // 2][:])

from contextlib import ExitStack

import concourse.mybir as mybir
from concourse.masks import make_identity

D, T, S, N, NQ = 512, 2048, 1024, 512, 256
FLOPS = 2 * D * N * NQ

F32 = mybir.dt.float32
BF16 = mybir.dt.bfloat16
U32 = mybir.dt.uint32
U16 = mybir.dt.uint16
U8 = mybir.dt.uint8
FP8X4 = mybir.dt.float8_e4m3fn_x4
ALU = mybir.AluOpType
ACT = mybir.ActivationFunctionType

P = 128
PACK = 4
HALF = N // 2
CW = 128
NCH = N // CW
POOL_END = CW + 32
LATE = 3 * CW


def tile_attend_pre_edge_f_topk_kernel(tc, qT, kT, rT, ob, offs, offs2, out):
    nc = tc.nc
    with ExitStack() as ctx:
        lists = ctx.enter_context(tc.tile_pool(name="lists", bufs=1))
        keep = ctx.enter_context(tc.tile_pool(name="keep", bufs=1))
        reuse = ctx.enter_context(tc.tile_pool(name="reuse", bufs=1))
        psum = ctx.enter_context(tc.psum_pool(name="psum", bufs=1))

        k_list = lists.tile([P, N // 16], U16, name="k_list")
        r_list = lists.tile([P, N // 16], U16, name="r_list")
        k_rows = kT.rearrange("(p t) s -> p t s", t=PACK)
        q_rows = qT[0].rearrange("(p t) q -> p t q", t=PACK)
        r_rows = rT.rearrange("(p t) s -> p t s", t=PACK)
        r_tab = [keep.tile([P, 2, S], F32, name=f"r_tab{j}", align_bytes=256) for j in range(2)]
        k_tab = [keep.tile([P, T], F32, name=f"k_tab{t}", align_bytes=256) for t in range(PACK)]
        q_raw = [reuse.tile([P, PACK, P], F32, name="q_raw0", align_bytes=256, offset=0), keep.tile([P, PACK, P], F32, name="q_raw1", align_bytes=256)]
        bias = [keep.tile([P, 1], F32, name=f"bias{h}") for h in range(2)]

        nc.sync.dma_start(r_tab[1][:], r_rows[:, 2:4, :])
        nc.sync.dma_start(r_list[:], offs2)
        nc.sync.dma_start(r_tab[0][:], r_rows[:, 0:2, :])
        nc.sync.dma_start(k_list[:], offs)
        for t in (3, 2, 1, 0):
            nc.sync.dma_start(k_tab[t][:], k_rows[:, t, :])
        for h in range(2):
            nc.sync.dma_start(q_raw[h][:], q_rows[:, :, h * P:(h + 1) * P])
        for h in range(2):
            nc.sync.dma_start(bias[h][:], ob[0, h * P:(h + 1) * P, :])

        ident = keep.tile([P, P], F32, name="ident")
        make_identity(nc, ident[:])
        r_g = keep.tile([P, PACK, N], F32, name="r_g")
        k_g = keep.tile([P, PACK, N], F32, name="k_g")
        u = keep.tile([P, LATE * PACK], BF16, name="u", align_bytes=64)
        u_late = keep.tile([P, CW * PACK], BF16, name="u_late", align_bytes=64)
        pairs = keep.tile([P, 2, CW * 2], BF16, name="pairs", align_bytes=64)
        u_v = u[:].rearrange("p (n t) -> p n t", t=PACK)
        q_bf = [keep.tile([P, P * PACK], BF16, name=f"q_bf{h}", align_bytes=64) for h in range(2)]
        u_codes = [keep.tile([P, CW], U32, name="u_codes0", align_bytes=256)]
        u_codes = u_codes + [reuse.tile([P, CW], U32, name=f"u_codes{c}", align_bytes=256, offset=4 * CW * c) for c in range(1, NCH)]
        u_scales = [keep.tile([P, 64 + CW], U8, name=f"u_scales{c}", align_bytes=256)[:, 64:] for c in range(NCH)]
        q_codes = [keep.tile([P, P], U32, name=f"q_codes{h}", align_bytes=256) for h in range(2)]
        q_scales = [keep.tile([P, 192 + P], U8, name=f"q_scales{h}", align_bytes=256)[:, 192:] for h in range(2)]
        res = [[keep.tile([P, HALF], F32, name=f"res{h}_{j}", align_bytes=256) for j in range(2)] for h in range(2)]

        def cols(c):
            return slice(c * CW, (c + 1) * CW)

        def gather_v(t, first, last):
            nc.vector.tensor_copy(k_g[:, t, first:last], k_tab[t][:].indirect(k_list[:, first // 16:last // 16]))

        def gather_s(t, first, last):
            nc.scalar.activation(k_g[:, t, first:last], k_tab[t][:].indirect(k_list[:, first // 16:last // 16]), ACT.Copy)

        def into_psum(t):
            turned = psum.tile([P, 3 * CW], F32, name=f"turned{t}", tag=f"bank{t}")
            held = keep.tile([P, 3 * CW], F32, name=f"held{t}")
            back = psum.tile([P, 3 * CW], F32, name=f"back{t}", tag=f"bank{7 - t}")
            for b in range(3):
                nc.tensor.transpose(turned[:, cols(b)], r_g[:, t, cols(b + 1)], ident[:])
            nc.scalar.copy(held[:], turned[:])
            for b in range(3):
                nc.tensor.transpose(back[:, cols(b)], held[:, cols(b)], ident[:])
            return back

        for t in (3, 2, 1, 0):
            nc.vector.tensor_copy(r_g[:, t, :], r_tab[t // 2][:, t % 2, :].indirect(r_list[:]))
        r_ps = {t: into_psum(t) for t in (1, 0)}

        def diff_v(t, first, last):
            nc.vector.tensor_tensor(u_v[:, first:last, t], k_g[:, t, first:last], r_ps[t][:, first - CW:last - CW], ALU.subtract)

        def diff_g(t, first, last):
            nc.gpsimd.tensor_tensor(u_v[:, first:last, t], k_g[:, t, first:last], r_g[:, t, first:last], ALU.subtract)

        def diff_late(t):
            nc.vector.tensor_tensor(pairs[:, 0, :].rearrange("p (n t) -> p n t", t=2)[:, :, t], k_g[:, t, LATE:N], r_ps[t][:, LATE - CW:N - CW], ALU.subtract)

        def diff_top(woven, first, last):
            nc.vector.tensor_tensor(woven.rearrange("p (c i) t -> p c t i", i=2), k_g[:, 2:4, first:last].rearrange("p t (c i) -> p c t i", i=2),
                                    r_g[:, 2:4, first:last].rearrange("p t (c i) -> p c t i", i=2), ALU.subtract)

        for t in (3, 2):
            gather_v(t, POOL_END, LATE)
            gather_s(t, LATE, N)
            gather_s(t, 0, POOL_END)
            if t == 2:
                diff_top(pairs[:, 1, :].rearrange("p (n t) -> p n t", t=2), LATE, N)
                diff_top(u_v[:, POOL_END:LATE, 2:4], POOL_END, LATE)
            diff_g(t, 0, POOL_END)

        gather_s(1, 0, POOL_END)
        gather_v(1, HALF, LATE)
        gather_s(1, LATE, N)
        gather_s(1, POOL_END, HALF)
        diff_g(1, 0, POOL_END)
        diff_v(1, HALF, LATE)
        diff_late(1)
        diff_v(1, POOL_END, HALF)

        gather_s(0, 0, POOL_END)
        gather_v(0, LATE, N)
        gather_v(0, HALF, LATE)
        gather_s(0, POOL_END, HALF)
        diff_g(0, 0, POOL_END)
        diff_late(0)
        diff_v(0, HALF, LATE)
        diff_v(0, POOL_END, HALF)

        def cast_q(h):
            nc.scalar.copy(q_bf[h][:].rearrange("p (c i t) -> p c t i", i=4, t=PACK), q_raw[h][:].rearrange("p t (c i) -> p c t i", i=4))

        cast_q(0)
        nc.scalar.copy(u_late[:].bitcast(U32).rearrange("p (c i w) -> p c w i", i=2, w=2),
                       pairs[:].rearrange("p w n -> p (w n)").bitcast(U32).rearrange("p (w c i) -> p c w i", w=2, i=2))
        cast_q(1)

        def quant_u(c):
            woven = u[:, c * CW * PACK:(c + 1) * CW * PACK] if c * CW < LATE else u_late[:]
            nc.vector.quantize_mx(out=u_codes[c][:].bitcast(FP8X4), scales=u_scales[c], in_=woven)

        def quant_q(h):
            nc.vector.quantize_mx(out=q_codes[h][:].bitcast(FP8X4), scales=q_scales[h], in_=q_bf[h][:])

        quant_u(0)
        quant_q(0)
        for c in range(1, NCH):
            quant_u(c)
        quant_q(1)

        for h in range(2):
            for c in range(NCH):
                acc = psum.tile([P, CW], F32, name=f"acc{h}_{c}", tag=f"bank{NCH * h + c}")
                nc.tensor.matmul_mx(out=acc[:], lhsT=q_codes[h][:].bitcast(FP8X4), lhsT_scale=q_scales[h],
                                    rhs=u_codes[c][:].bitcast(FP8X4), rhs_scale=u_scales[c], start=True, stop=True)
                dst = res[h][c // 2][:, cols(c % 2)]
                if h == 1 and c % 2 == 0:
                    nc.vector.tensor_scalar(dst, acc[:], bias[h][:], 0.0, ALU.add, ALU.max)
                else:
                    nc.scalar.activation(dst, acc[:], ACT.Relu, bias=bias[h][:])
                if c % 2 == 1:
                    nc.sync.dma_start(out[0, h * P:(h + 1) * P, (c // 2) * HALF:(c // 2 + 1) * HALF], res[h][c // 2][:])
